import numpy as np, ml_dtypes
CORES = [8,136,40,168]
N = 4
BF = ml_dtypes.bfloat16
VX, VY, C, B, LE = 2048, 2048, 192, 2, 6
def parts(rng):
    X = rng.integers(0, 256, (N, 8, 16, VX)); Y = rng.integers(0, 256, (N, 8, 16, VY))
    K = rng.integers(0, VX, (N, 8, 16, C)); G = rng.integers(0, VY, (N, 8, 16, B * C)); W = rng.integers(0, VX, (N, 8, 16, B * C))
    z = rng.integers(0, 256, (N, 8, 16, C)); w = rng.integers(0, 64, (N, 8, 16, 1)); t = rng.integers(1000, 1451, (N, 8, 16, 1))
    return X, Y, K, G, W, z, w, t
def pack(X, Y, K, G, W, z, w, t):
    fl = lambda a: np.ascontiguousarray(np.reshape(a, (N, 128, -1))).astype(np.float32).astype(BF)
    wh = lambda a: np.ascontiguousarray(np.reshape(a, (N, 128, -1))).astype(np.int32)
    return {"gx": fl(X), "sy": fl(Y), "rk": wh(K), "rt": wh(G), "wr": wh(W), "z0": fl(z), "wt": fl(w), "th": wh(t)}
def setup_inputs(rng):
    return pack(*parts(rng))
def uneven(rng, top, bits, shape):
    v = np.exp2(bits * rng.random(shape)).astype(np.int64) - 1
    return np.minimum(np.maximum(np.where(rng.random(shape) < 0.5, v, top - v), 0), top)
def setup_inputs_spread(rng):
    X, Y, K, G, W, z, w, t = parts(rng)
    X = (np.exp2(8 * rng.random((N, 8, 1, VX))) * rng.random(X.shape)).astype(np.int64)
    Y = (np.exp2(8 * rng.random((N, 8, 1, VY))) * rng.random(Y.shape)).astype(np.int64)
    z = (np.exp2(8 * rng.random((N, 8, 1, C))) * rng.random(z.shape)).astype(np.int64)
    lx = VX.bit_length() - 1; ly = VY.bit_length() - 1
    K = uneven(rng, VX - 1, lx, K.shape); W = uneven(rng, VX - 1, lx, W.shape); G = uneven(rng, VY - 1, ly, G.shape)
    w = uneven(rng, 63, 6, w.shape); t = rng.integers(0, 4081, t.shape)
    return pack(X, Y, K, G, W, z, w, t)
def setup_inputs_ends(rng):
    sh = np.array([0.0, 0.1, 0.5, 0.9, 1.0])
    X = 255 * (rng.random((N, 8, 16, VX)) < rng.choice(sh, (N, 8, 1, VX))); Y = 255 * (rng.random((N, 8, 16, VY)) < rng.choice(sh, (N, 8, 1, VY)))
    K = (VX - 1) * rng.integers(0, 2, (N, 8, 16, C)); G = (VY - 1) * rng.integers(0, 2, (N, 8, 16, B * C)); W = (VX - 1) * rng.integers(0, 2, (N, 8, 16, B * C))
    z = 255 * rng.integers(0, 2, (N, 8, 16, C)); w = 63 * rng.integers(0, 2, (N, 8, 16, 1)); t = 4080 * (rng.random((N, 8, 16, 1)) < 0.75)
    w[:, :, 0] = 63; w[:, 0, 1] = 0; t[:, 0] = 4080; t[:, 3, :4] = 0
    for q in range(N):
        for g in range(7):
            m = (q + g) % 4
            if m == 0: X[q, g, :, 0] = 0; X[q, g, :, VX - 1] = 255
            if m == 1: X[q, g, :, 0] = 255; X[q, g, :, VX - 1] = 0
            if m == 2: X[q, g, :, 0] = 255 * rng.integers(0, 2, 16); X[q, g, :, VX - 1] = 255
            if m == 3: X[q, g, :, 0] = 255 * rng.integers(0, 2, 16); X[q, g, :, VX - 1] = 255 * rng.integers(0, 2, 16)
    m1 = [m for m in range(1, 17) if (((((255 * 63 * m) & 4095) ** 2) >> 5) & (B - 1)) == B - 1][0]
    s1 = (VY - 1 + 37 * ((255 * 63 * m1) & 4095)) & (VY - 1)
    X[:, 7, :, 0] = 0; X[:, 7, :, VX - 1] = 255; Y[:, 7, :, 0] = 0; Y[:, 7, :, VY - 1] = 255; Y[:, 7, :, s1] = 255; w[:, 7] = 63; t[:, 7] = 4080
    for i, m in ((C - 1, m1), (C - 2, 0), (C - 3, 13), (C - 4, 16), (0, m1), (1, 0), (2, 16)):
        z[:, 7, :, i] = 255 * (np.arange(16) < m)
        K[:, 7, 15, i] = 0; K[:, 7, 14, i] = VX - 1; K[:, 7, 0, i] = 0; G[:, 7, 14:, B * i:B * i + B] = VY - 1; G[:, 7, 0, B * i:B * i + B] = VY - 1
    return pack(X, Y, K, G, W, z, w, t)
def setup_inputs_corners(rng):
    X, Y, K, G, W, z, w, t = parts(rng); h = VX // 2; v = VY // 4
    X[..., :h] = rng.integers(0, 48, (N, 8, 16, h)); X[..., h:] = rng.integers(208, 256, (N, 8, 16, VX - h)); Y[..., :v] = rng.integers(0, 48, (N, 8, 16, v))
    kind = rng.integers(0, 8, (N, 8, 1, C)); kind[..., :8] = np.arange(8); kind[..., C - 8:] = np.arange(8)
    k = np.arange(16)[:, None]; lane = rng.integers(0, 16, (N, 8, 1, C))
    up = ((kind == 1) & (k == 0)) | ((kind == 2) & (k == 15)) | ((kind == 3) & (k == lane)) | ((kind == 4) & (k <= lane))
    lh = np.where(up, rng.integers(h, VX, K.shape), rng.integers(0, h, K.shape))
    K = np.where(kind == 7, (VX - 1) * rng.integers(0, 2, K.shape), np.where(kind == 6, K, lh))
    z = np.where(kind < 5, rng.integers(64, 96, z.shape), np.where(kind == 5, 255, np.where(kind == 6, 0, z)))
    M = np.zeros((8, 16), np.int64); M[1] = 4080; M[7] = 4080; M[2, 15] = 4080; M[3, 0] = 4080; M[4, ::2] = 4080; M[5, :15] = 4080
    mode = (np.arange(N)[:, None] + np.arange(8)) % 8
    t = np.where((mode == 6)[:, :, None, None], rng.choice(np.array([0, 1, 4079, 4080, 1300]), t.shape), M[mode][..., None])
    q = rng.permutation(N); t[q[0]] = 0; t[q[1]] = 4080
    a = rng.integers(0, 3, (N, 8, 1, 1)); a[:, 0] = 0; a[:, 7] = 1; w = np.where(a == 0, 0, np.where(a == 1, 63, w))
    W = np.where(rng.random((N, 8, 1, 1)) < 0.4, (VX - 1) * rng.integers(0, 2, W.shape), W)
    G = np.where(rng.random((N, 8, 1, 1)) < 0.4, (VY - 1) * rng.integers(0, 2, G.shape), G)
    z[q[1], ::2] = 0
    e = int(q[2])
    X[e] = np.minimum(X[e], 254); Y[e] = rng.integers(0, 61, Y[e].shape); K[e] = rng.integers(0, h, K[e].shape); z[e] = 255; t[e] = rng.integers(2900, 3301, t[e].shape)
    b = int(q[3]); gb = (7 - b) % 8
    X[b, gb] = np.minimum(X[b, gb], 254); z[b, gb] = 255
    return pack(X, Y, K, G, W, z, w, t)
def setup_inputs_ties(rng):
    X, Y, K, G, W, z, w, t = parts(rng)
    X[:, ::2] = 128 * rng.integers(0, 2, (N, 4, 16, VX)); Y[:, ::2] = 128 * rng.integers(0, 2, (N, 4, 16, VY))
    X[:, 1::2] = 85 * rng.integers(0, 4, (N, 4, 16, VX)); Y[:, 1::2] = 85 * rng.integers(0, 4, (N, 4, 16, VY))
    z[:, ::2] = 16 * rng.integers(0, 9, (N, 4, 16, C)); z[:, 1::2] = np.maximum(85 * rng.integers(0, 4, (N, 4, 16, C)) - 16 * rng.integers(0, 8, (N, 4, 16, C)), 0)
    t[:, ::2] = 128 * rng.integers(6, 12, (N, 4, 16, 1)); t[:, 1::2] = 85 * rng.integers(17, 24, (N, 4, 16, 1))
    t = t + rng.integers(-1, 2, t.shape) * (rng.random(t.shape) < 0.5)
    X[:, 5] = rng.integers(200, 256, (N, 16, VX)); Y[:, 5] = rng.integers(0, 61, (N, 16, VY))
    X[:, 6] = rng.integers(0, 61, (N, 16, VX)); Y[:, 6] = rng.integers(200, 256, (N, 16, VY))
    t[:, 5:7] = 3160 + rng.integers(-300, 151, (N, 2, 16, 1))
    return pack(X, Y, K, G, W, z, w, t)
def setup_inputs_alike(rng):
    X, Y, K, G, W, z, w, t = parts(rng)
    K[:, ::2] = K[:, ::2, :1, :].copy(); K[:, 1] = K[:, 1, :, :1].copy(); W[:, 1] = W[:, 1, :, :1].copy()
    W[:, 2:4] = np.repeat(K[:, 2:4], B, axis=-1); G[:, 4] = G[:, 4, :1, :1].copy(); z[:, 5] = z[:, 5, :, :1].copy()
    few = np.array([0, VX - 1, VX // 2, 3]); K[:, 7] = rng.choice(few, (N, 16, C)); W[:, 7] = rng.choice(few, (N, 16, B * C))
    return pack(X, Y, K, G, W, z, w, t)
def check_inputs(d):
    bad = []
    for k, hi in (("gx", 255), ("sy", 255), ("rk", VX - 1), ("rt", VY - 1), ("wr", VX - 1), ("z0", 255), ("wt", 63), ("th", 4080)):
        a = np.asarray(d[k]).astype(np.float64)
        if not (np.min(a) >= 0 and np.max(a) <= hi): bad.append("range of " + k)
        elif not np.all(a == np.floor(a)): bad.append("whole numbers of " + k)
    return bad
def reference(gx, sy, rk, rt, wr, z0, wt, th):
    ints = lambda a, n: a.astype(np.float32).astype(np.int32).reshape(N, 8, 16, n)
    X, Y, z, w = ints(gx, VX), ints(sy, VY), ints(z0, C), ints(wt, 1)
    K = rk.astype(np.int64).reshape(N, 8, 16, C); G = rt.astype(np.int64).reshape(N, 8, 16, B * C); W = wr.astype(np.int64).reshape(N, 8, 16, B * C)
    t = th.astype(np.int64).reshape(N, 8, 16, 1); A = np.zeros((N, 1, 1, 1), np.int64)
    margin = (16 * ((15 - np.arange(16)) >> 1)).astype(np.int32)[:, None]
    for lead in range(LE):
        if lead > 0: K = np.roll(K, 1, axis=0); z = np.roll(z, 1, axis=0)
        u = np.add.reduce(w.astype(np.int64) * z, axis=2) & 4095
        c = B * np.arange(C) + (((u * u) >> 5) & (B - 1)); cc = np.broadcast_to(c[:, :, None, :], K.shape)
        route = np.take_along_axis(G, cc, 3); old = np.take_along_axis(W, cc, 3)
        s = (((route * K) >> 5) + route + 37 * u[:, :, None, :]) & (VY - 1)
        x = np.take_along_axis(X, K.reshape(N, 8, 1, 16 * C), 3).reshape(N, 8, 16, 16, C)
        y = np.take_along_axis(Y, s.reshape(N, 8, 1, 16 * C), 3).reshape(N, 8, 16, 16, C)
        placed = np.add.reduce(np.abs(x - y), axis=2) < t + A
        hold = placed & (np.count_nonzero(x >= z[:, :, :, None, :] + margin, axis=2) >= 9)
        stop = np.logical_or.accumulate(hold[:, :, ::-1], axis=2)[:, :, ::-1]
        held = placed & stop; fail = placed & ~stop
        h, f, o = held.astype(np.int64), fail.astype(np.int64), 1 - placed.astype(np.int64)
        nh = np.add.reduce(h, axis=2)[:, :, None]; nf = np.add.reduce(f, axis=2)[:, :, None]
        over = np.add.accumulate(h[:, :, ::-1], axis=2)[:, :, ::-1] - h
        pos = np.where(held, over, np.where(fail, nh + np.add.accumulate(f, axis=2) - f, nh + nf + np.add.accumulate(o, axis=2) - o))
        new = np.zeros_like(K); np.put_along_axis(new, pos, np.where(fail, old, K), 2)
        np.put_along_axis(W, cc, np.where(fail, K, old), 3)
        z = np.abs(z - np.maximum.reduce(np.where(held[:, :, None], x, 0), axis=3))
        A = 16 * (np.add.reduce(f, axis=(1, 2, 3)) & 31).reshape(N, 1, 1, 1)
        K = new
    return {"yk": K.reshape(N, 128, C).astype(np.float32), "yw": W.reshape(N, 128, B * C).astype(np.float32), "yz": z.reshape(N, 128, C).astype(np.float32).astype(BF)}

@@ -1,0 +1,660 @@
+from concourse.bass import DstId, RemoteDMATransfer
+from concourse.mybir import dt, AluOpType, AxisListType, ActivationFunctionType
+import math
+
+A = AluOpType
+AF = ActivationFunctionType
+LE = 6
+NC = 3
+CH = 64
+FULL = 16 * CH
+GAM = 1.5
+CY = 0.00083
+PC = 0.00042
+AHEAD = 0.0
+PER = 5.3
+BIAS = {}
+XP = 4
+SCB = True
+WAKE = 0.06
+
+SCRATCH = {
+    "gxb": ("sbuf", [128, 2048], "bfloat16"), "syb": ("sbuf", [128, 2048], "bfloat16"),
+    "rkb": ("sbuf", [128, 192], "int32"), "rtb": ("sbuf", [128, 384], "int32"), "wrb": ("sbuf", [128, 384], "int32"),
+    "wtb": ("sbuf", [128, 1], "bfloat16"), "thb": ("sbuf", [128, 1], "int32"),
+    "kin": ("sbuf", [128, LE * 192], "float16"), "zin": ("sbuf", [128, LE * 192], "bfloat16"),
+    "kout": ("sbuf", [128, LE * 192], "float16"), "zout": ("sbuf", [128, LE * 192], "bfloat16"),
+    "ykb": ("sbuf", [128, 192], "float32"), "ywb": ("sbuf", [128, 384], "float32"),
+    "pid": ("sbuf", [128, 1], "int32"), "pki": ("sbuf", [128, 1], "int32"), "pgi": ("sbuf", [128, 1], "int32"),
+    "mq": ("sbuf", [128, 128], "float32"), "mg": ("sbuf", [128, 128], "float32"), "mi": ("sbuf", [128, 128], "float32"),
+    "tq0": ("sbuf", [128, 128], "float32"),
+    "cols": ("sbuf", [128, 16], "float32"), "rmn": ("sbuf", [128, 16], "float32"), "rm1": ("sbuf", [128, 16], "float32"),
+    "w37": ("sbuf", [128, 1], "int32"), "w37l": ("sbuf", [128, 1], "int32"),
+    "mats": ("sbuf", [128, 24 * 128], "bfloat16"), "m16": ("sbuf", [128, 3 * 128], "float16"),
+    "bc": ("sbuf", [128, 2048], "bfloat16"), "bv": ("sbuf", [128, 2048], "float16"),
+    "bk": ("sbuf", [128, 2048], "bfloat16"), "tp": ("sbuf", [128, 2048], "bfloat16"),
+    "rst": ("sbuf", [128, 512], "bfloat16"),
+    "acc": ("sbuf", [128, 6], "float32"), "accb": ("sbuf", [128, 6], "bfloat16"),
+    "fi": ("sbuf", [128, 1], "int32"), "fj": ("sbuf", [128, 1], "int32"),
+    "ea0": ("psum", [128, 512], "float32"), "eb0": ("psum", [128, 512], "float32"),
+    "ea1": ("psum", [128, 512], "float32"), "eb1": ("psum", [128, 512], "float32"),
+    "ta": ("psum", [128, 512], "float32"), "tb": ("psum", [128, 512], "float32"),
+    "bf": ("psum", [128, 512], "float32"), "bm": ("psum", [128, 512], "float32"),
+}
+for _c in range(NC):
+    for _n, _w, _d in (("gw", 4 * CH, "float16"), ("ko", CH, "uint16"), ("so", CH, "uint16"), ("xg", FULL, "bfloat16"),
+                       ("dg", FULL, "bfloat16"), ("ab", FULL, "bfloat16"), ("cc", FULL, "float16"),
+                       ("ii", 4 * CH, "int32"), ("tt", 4 * CH, "int32"), ("hh", 4 * CH, "float16"), ("bd", 2 * CH, "float16"),
+                       ("sm", 12 * CH, "bfloat16")):
+        SCRATCH["%s%d" % (_n, _c)] = ("sbuf", [128, _w], _d)
+    for _n in ("ha", "hb", "ra", "rb", "eb"):
+        SCRATCH["%s%d" % ("e_" if _n == "eb" else _n, _c)] = ("sbuf", [128, 512], "bfloat16")
+
+LOADS = ["rk", "z0", "wt", "gx", "rt", "wr", "th", "sy"]
+SEMAPHORES = ["sv", "ss", "sp", "sg", "loc", "fin"] + ["ld_" + x for x in LOADS] + \
+    ["az%d_%d" % (e, c) for e in range(1, LE) for c in range(NC)] + ["ak%d_%d" % (e, c) for e in range(1, LE) for c in range(NC)]
+
+MAT = ["BLK", "I", "nI", "I16", "I256", "n32I", "GE", "U", "L", "LS", "US", "nU", "hU", "ONE", "nONE", "TQ", "W", "WH", "WL",
+       "I4", "IT", "x1", "x2"]
+COL = ["p", "k", "g", "b2", "b3", "pos", "kc", "thm", "thA", "wh", "wl"]
+SEM = {"V": "sv", "S": "ss", "P": "sp", "G": "sg"}
+
+
+def build():
+    ops = []
+    lastw, readers = {}, {}
+
+    def op(eng, name, cost, fn, R=(), W=(), banks=(), lat=0.0, sem=None):
+        k = len(ops)
+        deps, soft = set(), set()
+        for r in R:
+            if r in lastw:
+                deps.add(lastw[r])
+        for w in W:
+            if w in lastw:
+                deps.add(lastw[w])
+            for x in readers.get(w, ()):
+                soft.add(x)
+        o = {"k": k, "eng": eng, "name": name, "cost": cost, "fn": fn, "deps": deps, "soft": soft - deps, "banks": list(banks),
+             "lat": lat, "sem": sem}
+        ops.append(o)
+        for r in R:
+            readers.setdefault(r, []).append(k)
+        for w in W:
+            lastw[w] = k
+            readers[w] = []
+        return k
+
+    vc = lambda n: max(64, n) * CY
+    sc = lambda n: max(64, n) * CY
+    ga = lambda n: 0.05 + GAM * n * CY
+    mm = lambda n: n * 64 * PC
+    col = lambda T, n: T.cols[:, COL.index(n):COL.index(n) + 1]
+    mat = lambda T, n: T.mats[:, 128 * MAT.index(n):128 * MAT.index(n) + 128]
+    h16 = lambda T, n: T.m16[:, 128 * n:128 * n + 128]
+
+    for x, t in (("rk", 2.2), ("z0", 2.2), ("wt", 2.2), ("gx", 5.0), ("rt", 3.5), ("wr", 3.8), ("th", 3.0), ("sy", 7.0)):
+        op("N", "ld_" + x, t, None, W=["zin0_%d" % c for c in range(NC)] if x == "z0" else ["in_" + x], sem=("ld_" + x, 16))
+
+    op("G", "pid", 0.14, lambda g, T: g.iota(T.pid[:, 0:1], [[1, 1]], 0, 1), W=["pid"])
+    op("G", "mi", 0.35, lambda g, T: g.iota(T.mi[:], [[1, 128]], 0, 0, allow_small_or_imprecise_dtypes=True), W=["mi"])
+    op("G", "mg", 0.35, lambda g, T: g.iota(T.mg[:], [[1, 8], [0, 16]], 0, 0, allow_small_or_imprecise_dtypes=True), W=["mg"])
+    op("G", "mq", 0.35, lambda g, T: g.iota(T.mq[:], [[0, 8], [1, 16]], 0, 0, allow_small_or_imprecise_dtypes=True), W=["mq"])
+    V = lambda name, n, fn, R=(), W=(), banks=(), cost=None: op("V", name, vc(n) if cost is None else cost, fn, R, W, banks)
+    S = lambda name, n, fn, R=(), W=(), banks=(), cost=None: op("S", name, sc(n) if cost is None else cost, fn, R, W, banks)
+    P = lambda name, n, fn, R=(), W=(), banks=(): op("P", name, mm(n), fn, R, W, banks)
+    V("pki", 1, lambda g, T: g.vector.tensor_scalar(T.pki[:, 0:1], T.pid[:, 0:1], 15, None, A.bitwise_and), ["pid"], ["pki"])
+    V("pgi", 1, lambda g, T: g.vector.tensor_scalar(T.pgi[:, 0:1], T.pid[:, 0:1], 4, None, A.arith_shift_right), ["pid"], ["pgi"])
+    V("cp", 1, lambda g, T: g.vector.tensor_copy(col(T, "p"), T.pid[:, 0:1]), ["pid"], ["c_p"])
+    V("cg", 1, lambda g, T: g.vector.tensor_copy(col(T, "g"), T.pgi[:, 0:1]), ["pgi"], ["c_g"])
+    V("ck", 1, lambda g, T: g.vector.tensor_copy(col(T, "k"), T.pki[:, 0:1]), ["pki"], ["c_k"])
+    V("BLK", 128, lambda g, T: g.vector.tensor_scalar(mat(T, "BLK"), T.mg[:], col(T, "g"), None, A.is_equal), ["mg", "c_g"], ["BLK"])
+    V("W", 64, lambda g, T: g.vector.tensor_scalar(mat(T, "W"), mat(T, "BLK"), T.wtb[:, 0:1], None, A.mult), ["BLK", "in_wt"], ["W"])
+
+    def diag(name, s):
+        V(name, 128, lambda g, T: g.vector.tensor_scalar(mat(T, name), T.mi[:], col(T, "p"), float(s), A.is_equal, A.mult),
+          ["mi", "c_p"], [name])
+    diag("I", 1.0)
+    for j, s in enumerate((1.0, -1.0, -2.0)):
+        V("H%d" % j, 128, lambda g, T, j=j, s=s: g.vector.tensor_scalar(h16(T, j), T.mi[:], col(T, "p"), s, A.is_equal, A.mult),
+          ["mi", "c_p"], ["H%d" % j])
+    V("w37", 1, lambda g, T: g.vector.tensor_scalar(T.w37[:, 0:1], T.wtb[:, 0:1], 37.0, None, A.mult), ["in_wt"], ["w37"])
+    V("w37l", 1, lambda g, T: g.vector.tensor_scalar(T.w37l[:, 0:1], T.w37[:, 0:1], 15, None, A.bitwise_and), ["w37"], ["w37l"])
+    V("wl", 1, lambda g, T: g.vector.tensor_copy(col(T, "wl"), T.w37l[:, 0:1]), ["w37l"], ["c_wl"])
+    V("wh", 1, lambda g, T: g.vector.tensor_tensor(col(T, "wh"), T.w37[:, 0:1], T.w37l[:, 0:1], A.subtract), ["w37", "w37l"], ["c_wh"])
+    V("WH", 64, lambda g, T: g.vector.tensor_scalar(mat(T, "WH"), mat(T, "BLK"), col(T, "wh"), None, A.mult), ["BLK", "c_wh"], ["WH"])
+    V("WL", 64, lambda g, T: g.vector.tensor_scalar(mat(T, "WL"), mat(T, "BLK"), col(T, "wl"), None, A.mult), ["BLK", "c_wl"], ["WL"])
+    diag("nI", -1.0)
+    V("rmn", 16, lambda g, T: g.vector.tensor_scalar(T.rmn[:], T.mq[:, 0:16], col(T, "k"), -512.0, A.is_equal, A.mult), ["mq", "c_k"], ["rmn"])
+    V("rm1", 16, lambda g, T: g.vector.tensor_scalar(T.rm1[:], T.mq[:, 0:16], col(T, "k"), None, A.is_equal), ["mq", "c_k"], ["rm1"])
+    for k in range(16):
+        S("bc%d" % k, 128, lambda g, T, k=k: g.scalar.activation(T.bc[:, 128 * k:128 * k + 128], mat(T, "BLK"), AF.Copy,
+                                                                 scale=T.rmn[:, k:k + 1]), ["BLK", "rmn"], ["bc%d" % k])
+    diag("IT", -1.0 / 512)
+    for q in range(4):
+        def trs(g, T, q=q):
+            o = T.ta if q % 2 == 0 else T.tb
+            for j in range(4):
+                k = 4 * q + j
+                r = g.tensor.matmul(o[:, 128 * j:128 * j + 128], T.bc[:, 128 * k:128 * k + 128], mat(T, "IT"), True, True)
+            return r
+        b = "ta" if q % 2 == 0 else "tb"
+        P("trs%d" % q, 8, trs, ["IT"] + ["bc%d" % k for k in range(4 * q, 4 * q + 4)], ["p_" + b], [b])
+        S("bk%d" % q, 512, lambda g, T, q=q: g.scalar.activation(T.bk[:, 512 * q:512 * q + 512], (T.ta if q % 2 == 0 else T.tb)[:], AF.Copy),
+          ["p_" + b], ["bk%d" % q], [b])
+    diag("I16", 16.0)
+    diag("I256", 256.0)
+    diag("n32I", -32.0)
+    V("GE0", 128, lambda g, T: g.vector.tensor_scalar(mat(T, "x1"), T.mi[:], col(T, "p"), None, A.is_le), ["mi", "c_p"], ["x1"])
+    tt = lambda name, a, b, o: V(name, 256, lambda g, T: g.vector.tensor_tensor(mat(T, name), mat(T, a), mat(T, b), o), [a, b], [name])
+    tt("GE", "x1", "BLK", A.mult)
+    tt("U", "GE", "I", A.subtract)
+    tt("L", "BLK", "GE", A.subtract)
+    V("x2", 64, lambda g, T: g.vector.tensor_scalar(mat(T, "x2"), mat(T, "L"), 0.5, None, A.mult), ["L"], ["x2"])
+    tt("LS", "x2", "n32I", A.subtract)
+    tt("US", "U", "I16", A.subtract)
+    V("nU", 64, lambda g, T: g.vector.tensor_scalar(mat(T, "nU"), mat(T, "U"), -1.0, None, A.mult), ["U"], ["nU"])
+    V("hU", 64, lambda g, T: g.vector.tensor_scalar(mat(T, "hU"), mat(T, "U"), -0.5, None, A.mult), ["U"], ["hU"])
+    for n, a, b in (("b2", 0.5, -32.0), ("b3", 1.0, -16.0), ("pos", -1.0, 16.0), ("kc", 2048.0, -30720.0)):
+        V("c_" + n, 1, lambda g, T, n=n, a=a, b=b: g.vector.tensor_scalar(col(T, n), col(T, "k"), a, b, A.mult, A.add), ["c_k"], ["c_" + n])
+    V("thm", 1, lambda g, T: g.vector.tensor_scalar(col(T, "thm"), T.thb[:, 0:1], -0.5, None, A.add), ["in_th"], ["c_thm"])
+    V("ONE", 64, lambda g, T: g.vector.memset(mat(T, "ONE"), 1.0), [], ["ONE"])
+    V("nONE", 64, lambda g, T: g.vector.memset(mat(T, "nONE"), -1.0), [], ["nONE"])
+    V("rst0", 256, lambda g, T: g.vector.memset(T.rst[:], 1.0), [], ["rst"])
+    V("rst1", 64, lambda g, T: g.vector.memset(T.rst[:, 0::8], 0.0), [], ["rst"])
+    V("tq0", 128, lambda g, T: g.vector.tensor_scalar(T.tq0[:], T.mq[:], -16.0, -8.0, A.mult, A.add), ["mq"], ["tq0"])
+    V("TQ", 256, lambda g, T: g.vector.tensor_tensor(mat(T, "TQ"), T.tq0[:], mat(T, "BLK"), A.mult), ["tq0", "BLK"], ["TQ"])
+    diag("I4", -4.0)
+    for k in range(16):
+        V("bv%d" % k, 64, lambda g, T, k=k: g.vector.tensor_scalar(T.bv[:, 128 * k:128 * k + 128], mat(T, "BLK"), T.rm1[:, k:k + 1], None, A.mult),
+          ["BLK", "rm1"], ["bv%d" % k])
+    for q in range(4):
+        def tps(g, T, q=q):
+            o = T.ta if q % 2 == 0 else T.tb
+            for j in range(4):
+                k = 4 * q + j
+                g.tensor.matmul(o[:, 128 * j:128 * j + 128], mat(T, "I4"), T.bc[:, 128 * k:128 * k + 128], True, False)
+                r = g.tensor.matmul(o[:, 128 * j:128 * j + 128], mat(T, "I"), mat(T, "TQ"), False, True)
+            return r
+        b = "ta" if q % 2 == 0 else "tb"
+        P("tps%d" % q, 16, tps, ["I", "I4", "TQ"] + ["bc%d" % k for k in range(4 * q, 4 * q + 4)], ["p_" + b, "p_" + b + "0", "p_" + b + "1"], [b])
+        S("tp%d" % q, 512, lambda g, T, q=q: g.scalar.activation(T.tp[:, 512 * q:512 * q + 512], (T.ta if q % 2 == 0 else T.tb)[:], AF.Copy),
+          ["p_" + b, "p_" + b + "0", "p_" + b + "1"], ["tp%d" % q], [b])
+
+    for c in range(NC):
+        sl = slice(CH * c, CH * c + CH)
+        V("k0_%d" % c, CH, lambda g, T, sl=sl: g.vector.tensor_copy(T.kin[:, sl], T.rkb[:, sl]), ["in_rk"], ["kin0_%d" % c])
+        ev, od = slice(2 * CH * c, 2 * CH * c + 2 * CH, 2), slice(2 * CH * c + 1, 2 * CH * c + 2 * CH, 2)
+        for src, base, dif in (("rt", 3, 0), ("wr", 2, 1)):
+            V("%sb%d" % (src, c), CH, lambda g, T, c=c, src=src, base=base, ev=ev:
+              g.vector.tensor_copy(T["gw%d" % c][:, CH * base:CH * base + CH], T[src + "b"][:, ev]), ["in_" + src], ["gw%d_%d" % (base, c)])
+            V("%sd%d" % (src, c), 2 * CH, lambda g, T, c=c, src=src, dif=dif, ev=ev, od=od:
+              g.vector.tensor_tensor(T["gw%d" % c][:, CH * dif:CH * dif + CH], T[src + "b"][:, od], T[src + "b"][:, ev], A.subtract),
+              ["in_" + src], ["gw%d_%d" % (dif, c)])
+
+    fr = lambda T, j, n=1: T.bf[:, 64 * j:64 * j + 64 * n]
+    mr = lambda T, j, n=1: T.bm[:, 64 * j:64 * j + 64 * n]
+    for e in range(LE):
+        for c in range(NC):
+            n = NC * e + c
+            es = str(n % 2)
+            base = 192 * e + CH * c
+            kin = lambda T, b=base: T.kin[:, b:b + CH]
+            zin = lambda T, b=base: T.zin[:, b:b + CH]
+            K_, Z_ = "kin%d_%d" % (e, c), "zin%d_%d" % (e, c)
+            t = lambda x, c=c: "%s%d" % (x, c)
+            sm = lambda T, j, c=c: T["sm%d" % c][:, CH * j:CH * j + CH]
+            ii = lambda T, j, c=c: T["ii%d" % c][:, CH * j:CH * j + CH]
+            tb = lambda T, j, c=c: T["tt%d" % c][:, CH * j:CH * j + CH]
+            hh = lambda T, j, c=c: T["hh%d" % c][:, CH * j:CH * j + CH]
+            gw = lambda T, j, m=1, c=c: T["gw%d" % c][:, CH * j:CH * j + CH * m]
+            nm = lambda x, e=e, c=c: "%s.%d.%d" % (x, e, c)
+            if e > 0:
+                op("N", nm("az"), 2.5, None, R=["sentz%d_%d" % (e, c)], W=[Z_], sem=("az%d_%d" % (e, c), 0))
+                op("N", nm("ak"), 2.5, None, R=["sentk%d_%d" % (e, c)], W=[K_], sem=("ak%d_%d" % (e, c), 0))
+            V(nm("ko"), CH, lambda g, T, t=t, kin=kin: g.vector.tensor_copy(T[t("ko")][:], kin(T)), [K_], [t("ko")])
+            for q in range(XP):
+                a, b = FULL // XP * q, FULL // XP * (q + 1)
+                S(nm("xg%d" % q), 0, lambda g, T, t=t, q=q, a=a, b=b: g.scalar.activation(
+                    T[t("xg")][:, a:b], T.gxb[:].indirect(T[t("ko")][:, a // 16:b // 16]), AF.Copy),
+                  [t("ko"), "in_gx"], [t("xg") + "_%d" % q], cost=0.065 + GAM * FULL // XP * CY)
+            XG = [t("xg") + "_%d" % q for q in range(XP)]
+            P(nm("U"), 1, lambda g, T, zin=zin: g.tensor.matmul(fr(T, 0), mat(T, "W"), zin(T), True, True), [Z_, "W"], ["f0"], ["bf"])
+            V(nm("r1"), CH, lambda g, T, ii=ii: g.vector.tensor_copy(ii(T, 0), fr(T, 0)), ["f0"], [t("ii0")], ["bf"])
+            V(nm("r2"), CH, lambda g, T, ii=ii: g.vector.tensor_scalar(ii(T, 1), ii(T, 0), 63, None, A.bitwise_and), [t("ii0")], [t("ii1")])
+            V(nm("r3"), 2 * CH, lambda g, T, ii=ii: g.vector.tensor_tensor(ii(T, 2), ii(T, 1), ii(T, 1), A.mult), [t("ii1")], [t("ii2")])
+            V(nm("r4"), CH, lambda g, T, ii=ii: g.vector.tensor_scalar(ii(T, 3), ii(T, 2), 5, 1, A.arith_shift_right, A.bitwise_and),
+              [t("ii2")], [t("ii3")])
+            V(nm("r5"), CH, lambda g, T, ii=ii, hh=hh: g.vector.tensor_copy(hh(T, 3), ii(T, 3)), [t("ii3")], [t("b")])
+
+            def fb(g, T, hh=hh):
+                g.tensor.matmul(fr(T, 1), h16(T, 0), hh(T, 3), True, True)
+                return g.tensor.matmul(fr(T, 2), h16(T, 0), hh(T, 3), True, True)
+            P(nm("fb"), 2, fb, [t("b"), "H0"], ["f1"], ["bf"])
+            V(nm("bd"), 2 * CH, lambda g, T, t=t, gw=gw: g.vector.tensor_tensor(T[t("bd")][:], gw(T, 0, 2), fr(T, 1, 2), A.mult),
+              ["f1", t("gw0_"), t("gw1_")], [t("bd")], ["bf"])
+
+            def rq(g, T, t=t, gw=gw, zin=zin):
+                i = h16(T, 0)
+                g.tensor.matmul(fr(T, 3), i, gw(T, 3), True, False)
+                g.tensor.matmul(fr(T, 3), i, T[t("bd")][:, 0:CH], False, True)
+                g.tensor.matmul(fr(T, 5), mat(T, "WH"), zin(T), True, False)
+                g.tensor.matmul(fr(T, 5), mat(T, "WL"), zin(T), False, False)
+                g.tensor.matmul(fr(T, 5), i, gw(T, 3), False, False)
+                r = g.tensor.matmul(fr(T, 5), i, T[t("bd")][:, 0:CH], False, True)
+                return r
+
+            def od(g, T, t=t, gw=gw, kin=kin):
+                i = h16(T, 0)
+                g.tensor.matmul(fr(T, 4), i, gw(T, 2), True, False)
+                g.tensor.matmul(fr(T, 4), h16(T, 1), kin(T), False, False)
+                return g.tensor.matmul(fr(T, 4), i, T[t("bd")][:, CH:2 * CH], False, True)
+            P(nm("rq"), 6, rq, [t("bd"), t("gw3_"), Z_, "H0", "WH", "WL"], ["f3", "f5"], ["bf"])
+            V(nm("t1"), CH, lambda g, T, tb=tb, kin=kin: g.vector.tensor_tensor(tb(T, 0), fr(T, 3), kin(T), A.mult), ["f3", K_], [t("t0")], ["bf"])
+            V(nm("t2"), CH, lambda g, T, tb=tb: g.vector.tensor_scalar(tb(T, 1), tb(T, 0), 5, None, A.arith_shift_right), [t("t0")], [t("t1")])
+            V(nm("t3"), CH, lambda g, T, tb=tb: g.vector.tensor_tensor(tb(T, 2), fr(T, 5), tb(T, 1), A.add), [t("t1"), "f5"], [t("t2")], ["bf"])
+            V(nm("t4"), CH, lambda g, T, tb=tb: g.vector.tensor_scalar(tb(T, 3), tb(T, 2), 2047, None, A.bitwise_and), [t("t2")], [t("t3")])
+            V(nm("so"), CH, lambda g, T, t=t, tb=tb: g.vector.tensor_copy(T[t("so")][:], tb(T, 3)), [t("t3")], [t("so")])
+            for q in range(XP):
+                a, b = FULL // XP * q, FULL // XP * (q + 1)
+                V(nm("dg%d" % q), 0, lambda g, T, t=t, q=q, a=a, b=b: g.vector.tensor_tensor(
+                    T[t("dg")][:, a:b], T.syb[:].indirect(T[t("so")][:, a // 16:b // 16]), T[t("xg")][:, a:b], A.subtract),
+                  [t("so"), t("xg") + "_%d" % q, "in_sy"], [t("dg") + "_%d" % q], cost=ga(FULL // XP))
+                S(nm("ab%d" % q), FULL // XP, lambda g, T, t=t, a=a, b=b: g.scalar.activation(T[t("ab")][:, a:b], T[t("dg")][:, a:b], AF.Abs),
+                  [t("dg") + "_%d" % q], [t("ab") + "_%d" % q])
+            for bank, k0, hb in (("ea0", 0, "ha"), ("eb0", 8, "hb")):
+                def ez(g, T, bank=bank, k0=k0, t=t, zin=zin):
+                    for kk in range(8):
+                        o = T[bank][:, CH * kk:CH * kk + CH]
+                        g.tensor.matmul(o, mat(T, "I"), T[t("xg")][:, k0 + kk::16], True, False)
+                        r = g.tensor.matmul(o, mat(T, "nI"), zin(T), False, True)
+                    return r
+                P(nm("E" + bank[:2]), 16, ez, XG + [Z_, "I", "nI"], ["p_" + bank], [bank])
+                for a in range(2):
+                    def sgn(g, T, bank=bank, hb=hb, a=a, t=t, k0=k0):
+                        for kk in (4 * a, 4 * a + 2):
+                            m = 16 * ((15 - (k0 + kk)) // 2)
+                            r = g.scalar.activation(T[t(hb)][:, CH * kk:CH * kk + 2 * CH], T[bank][:, CH * kk:CH * kk + 2 * CH], AF.Sign, bias=0.5 - m)
+                        return r
+                    S(nm("sg%s%d" % (bank[:2], a)), 4 * CH, sgn, ["p_" + bank], [t(hb) + "_%d" % a], [bank])
+            EB = [("ea1", 0), ("eb1", 8)]
+            for bank, k0 in EB:
+                def ex(g, T, bank=bank, k0=k0, t=t):
+                    for kk in range(8):
+                        r = g.tensor.matmul(T[bank][:, kk::8], mat(T, "I"), T[t("xg")][:, k0 + kk::16], kk == 0, False)
+                    return r
+                P(nm("X" + bank[:2]), 8, ex, XG + ["I"], ["p_" + bank], [bank])
+
+            def dsum(g, T, t=t):
+                for k in range(16):
+                    r = g.tensor.matmul(fr(T, 6), T.bk[:, 128 * k:128 * k + 128], T[t("ab")][:, k::16], k == 0, k == 15)
+                return r
+            P(nm("ds"), 16, dsum, [t("ab") + "_%d" % q for q in range(XP)] + ["bk%d" % q for q in range(4)], ["f6"], ["bf"])
+
+            def hsum(g, T, t=t):
+                for k in range(16):
+                    r = g.tensor.matmul(mr(T, 0), T.bk[:, 128 * k:128 * k + 128], T[t("ha" if k < 8 else "hb")][:, CH * (k % 8):CH * (k % 8) + CH], k == 0, k == 15)
+                return r
+            P(nm("hs"), 16, hsum, [t(x) + "_%d" % a for x in ("ha", "hb") for a in range(2)] + ["bk%d" % q for q in range(4)], ["m0"], ["bm"])
+            th = "c_thm" if e == 0 else "c_thA"
+            S(nm("hr"), CH, lambda g, T, sm=sm: g.scalar.activation(sm(T, 0), mr(T, 0), AF.Relu), ["m0"], [t("hr")], ["bm"])
+            S(nm("sp"), CH, lambda g, T, sm=sm, e=e, c=c: g.scalar.activation(
+                sm(T, 1), fr(T, 6), AF.Sign, scale=-1.0, bias=col(T, "thm" if e == 0 else "thA"), accum_out=T.acc[:, c:c + 1]),
+              ["f6", th], [t("sp"), "acc%d" % c], ["bf"])
+
+            def h2(g, T, sm=sm):
+                g.tensor.matmul(mr(T, 1), mat(T, "I"), sm(T, 0), True, False)
+                return g.tensor.matmul(mr(T, 1), mat(T, "I16"), sm(T, 1), False, True)
+            P(nm("h2"), 2, h2, [t("hr"), t("sp"), "I", "I16"], ["m1"], ["bm"])
+            S(nm("hp"), CH, lambda g, T, sm=sm: g.scalar.activation(sm(T, 2), mr(T, 1), AF.Relu, bias=-16.0), ["m1"], [t("hp")], ["bm"])
+
+            def vs(g, T, sm=sm):
+                g.tensor.matmul(mr(T, 2), mat(T, "GE"), sm(T, 2), True, False)
+                return g.tensor.matmul(mr(T, 2), mat(T, "I256"), sm(T, 1), False, True)
+            P(nm("vs"), 2, vs, [t("hp"), t("sp"), "GE", "I256"], ["m2"], ["bm"])
+            S(nm("sg"), CH, lambda g, T, sm=sm, c=c: g.scalar.activation(sm(T, 3), mr(T, 2), AF.Sign, bias=-256.0,
+                                                                        accum_out=T.acc[:, 3 + c:4 + c]),
+              ["m2"], [t("sg"), "acc%d" % (3 + c)], ["bm"])
+
+            def bb(g, T, sm=sm, hh=hh, kin=kin):
+                s, p = sm(T, 3), sm(T, 1)
+                g.tensor.matmul(mr(T, 3), mat(T, "LS"), p, True, False)
+                g.tensor.matmul(mr(T, 3), mat(T, "n32I"), s, False, True)
+                g.tensor.matmul(mr(T, 4), mat(T, "US"), p, True, False)
+                return g.tensor.matmul(mr(T, 4), mat(T, "nU"), s, False, True)
+            P(nm("bb"), 4, bb, [t("sg"), t("sp"), "LS", "n32I", "US", "nU"], ["m3", "m4"], ["bm"])
+            P(nm("od"), 3, od, [t("bd"), t("gw2_"), K_, "H0", "H1", t("sp")], ["f4"], ["bf"])
+            P(nm("kp"), 1, lambda g, T, kin=kin: g.tensor.matmul(mr(T, 5), h16(T, 0), kin(T), True, True), [K_, "H0", t("sg")], ["m5"], ["bm"])
+            S(nm("f0"), CH, lambda g, T, sm=sm: g.scalar.activation(sm(T, 10), sm(T, 3), AF.Abs), [t("sg")], [t("fa")])
+            S(nm("f1"), CH, lambda g, T, sm=sm: g.scalar.activation(sm(T, 11), sm(T, 10), AF.Copy, scale=-1.0, bias=1.0), [t("fa")], [t("fl")])
+            S(nm("R2"), CH, lambda g, T, sm=sm: g.scalar.activation(sm(T, 4), mr(T, 3), AF.Relu, bias=col(T, "b2")), ["m3", "c_b2"], [t("R2")], ["bm"])
+            S(nm("R3"), CH, lambda g, T, sm=sm: g.scalar.activation(sm(T, 5), mr(T, 4), AF.Relu, bias=col(T, "b3")), ["m4", "c_b3"], [t("R3")], ["bm"])
+            V(nm("fd"), CH, lambda g, T, hh=hh, sm=sm: g.vector.tensor_tensor(hh(T, 1), fr(T, 4), sm(T, 11), A.mult), ["f4", t("fl")], [t("fd")], ["bf"])
+            V(nm("v"), CH, lambda g, T, t=t, hh=hh: g.vector.tensor_tensor(T[t("vv")][:], mr(T, 5), hh(T, 1), A.add), ["m5", t("fd")], [t("v")], ["bm"])
+
+            def po(g, T, sm=sm):
+                g.tensor.matmul(mr(T, 6), mat(T, "U"), sm(T, 3), True, False)
+                g.tensor.matmul(mr(T, 6), mat(T, "hU"), sm(T, 1), False, False)
+                g.tensor.matmul(mr(T, 6), mat(T, "I"), sm(T, 4), False, False)
+                return g.tensor.matmul(mr(T, 6), mat(T, "I"), sm(T, 5), False, True)
+            P(nm("po"), 4, po, [t("sg"), t("sp"), t("R2"), t("R3"), "U", "hU", "I"], ["m6"], ["bm"])
+            S(nm("nu"), CH, lambda g, T, sm=sm: g.scalar.activation(sm(T, 7), sm(T, 3), AF.Copy, scale=-1.0, bias=1.0), [t("sg")], [t("nu")])
+            S(nm("pp"), CH, lambda g, T, sm=sm: g.scalar.activation(sm(T, 6), mr(T, 6), AF.Identity, scale=2.0, bias=col(T, "pos")),
+              ["m6", "c_pos"], [t("pp")], ["bm"])
+            for bank, k0 in EB:
+                def mk(g, T, bank=bank, k0=k0, sm=sm):
+                    for kk in range(8):
+                        k = k0 + kk
+                        r = g.tensor.matmul(T[bank][:, kk::8], T.bc[:, 128 * k:128 * k + 128], sm(T, 7), False, kk == 7)
+                    return r
+                P(nm("mk" + bank[:2]), 8, mk, [t("nu")] + ["bc%d" % k for k in range(k0, k0 + 8)], ["p_" + bank], [bank])
+            bA, bB = EB[0][0], EB[1][0]
+            for a, b in ((0, 256), (256, 512)):
+                V(nm("sca%d" % (a > 0)), 256, lambda g, T, t=t, bA=bA, a=a, b=b: g.vector.tensor_tensor_scan(
+                    T[t("ra")][:, a:b], T.rst[:, a:b], T[bA][:, a:b], 0.0, A.mult, A.max), ["p_" + bA, "rst"], [t("ra") + "_%d" % (a > 0)], [bA])
+            if SCB:
+                S(nm("eb"), 512, lambda g, T, t=t, bB=bB: g.scalar.activation(T[t("e_")][:], T[bB][:], AF.Copy), ["p_" + bB], [t("e_")], [bB])
+                V(nm("scb"), 256, lambda g, T, t=t: g.vector.tensor_tensor_scan(T[t("rb")][:], T.rst[:], T[t("e_")][:], 0.0, A.mult, A.max),
+                  [t("e_"), "rst"], [t("rb")])
+            else:
+                V(nm("scb"), 512, lambda g, T, t=t, bB=bB: g.vector.tensor_tensor_scan(T[t("rb")][:], T.rst[:], T[bB][:], 0.0, A.mult, A.max),
+                  ["p_" + bB, "rst"], [t("rb")], [bB])
+            P(nm("nz"), 1, lambda g, T, zin=zin: g.tensor.matmul(mr(T, 4), mat(T, "nI"), zin(T), True, True), [Z_, "nI", t("R3")], ["m4"], ["bm"])
+            V(nm("m1"), 2 * CH, lambda g, T, t=t, sm=sm: g.vector.tensor_tensor(sm(T, 8), T[t("ra")][:, 7::8], T[t("rb")][:, 7::8], A.max),
+              [t("ra") + "_0", t("ra") + "_1", t("rb")], [t("mx")])
+            V(nm("m2"), CH, lambda g, T, sm=sm: g.vector.tensor_tensor(sm(T, 9), mr(T, 4), sm(T, 8), A.add), [t("mx"), "m4"], [t("my")], ["bm"])
+            last = e == LE - 1
+            S(nm("za"), CH, lambda g, T, sm=sm, base=base: g.scalar.activation(T.zout[:, base:base + CH], sm(T, 9), AF.Abs),
+              [t("my")], ["zout%d_%d" % (e, c)])
+            if not last:
+                op("G", nm("sz"), 1.0, ("send", "z", e, c, base), R=["zout%d_%d" % (e, c)], W=["sentz%d_%d" % (e + 1, c)])
+            else:
+                op("Y", nm("yz"), 0.1, lambda g, T, base=base, c=c: g.sync.dma_start(T.yz[:, CH * c:CH * c + CH], T.zout[:, base:base + CH]),
+                   R=["zout%d_%d" % (e, c)], W=["yz%d" % c], lat=2.0)
+            for h in range(4):
+                bank, lo = ("ta", "tb")[h % 2], 256 * (h // 2)
+
+                def tk(g, T, h=h, bank=bank, lo=lo, sm=sm, t=t):
+                    for kk in range(4):
+                        k = 4 * h + kk
+                        o = T[bank][:, lo + CH * kk:lo + CH * kk + CH]
+                        g.tensor.matmul(o, T.tp[:, 128 * k:128 * k + 128], sm(T, 6), True, False)
+                        r = g.tensor.matmul(o, T.bv[:, 128 * k:128 * k + 128], T[t("vv")][:], False, True)
+                    return r
+                P(nm("T%d" % h), 8, tk, [t("pp"), t("v"), "tp%d" % h] + ["bv%d" % k for k in range(4 * h, 4 * h + 4)],
+                  ["p_%s%d" % (bank, h // 2)], [bank])
+                V(nm("cl%d" % h), 256, lambda g, T, bank=bank, lo=lo, h=h, t=t: g.vector.tensor_scalar(
+                    T[t("cc")][:, 256 * h:256 * h + 256], T[bank][:, lo:lo + 256], 0.0, 2048.0, A.max, A.min),
+                  ["p_%s%d" % (bank, h // 2)], [t("cc") + "_%d" % h], [bank])
+
+            def cs(g, T, t=t):
+                for k in range(16):
+                    r = g.tensor.matmul(mr(T, 7), h16(T, 0), T[t("cc")][:, CH * k:CH * k + CH], k == 0, k == 15)
+                return r
+            P(nm("cs"), 16, cs, [t("cc") + "_%d" % h for h in range(4)] + ["H0"], ["m7"], ["bm"])
+            if not last:
+                V(nm("kn"), CH, lambda g, T, base=base: g.vector.tensor_scalar(T.kout[:, base:base + CH], mr(T, 7), col(T, "kc"), None, A.add),
+                  ["m7", "c_kc"], ["kout%d_%d" % (e, c)], ["bm"])
+                op("G", nm("sk"), 1.0, ("send", "k", e, c, base), R=["kout%d_%d" % (e, c)], W=["sentk%d_%d" % (e + 1, c)])
+            else:
+                V(nm("kn"), CH, lambda g, T, c=c: g.vector.tensor_scalar(T.ykb[:, CH * c:CH * c + CH], mr(T, 7), col(T, "kc"), None, A.add),
+                  ["m7", "c_kc"], ["ykb%d" % c], ["bm"])
+                op("Y", nm("yk"), 0.1, lambda g, T, c=c: g.sync.dma_start(T.yk[:, CH * c:CH * c + CH], T.ykb[:, CH * c:CH * c + CH]),
+                   R=["ykb%d" % c], W=["yk%d" % c], lat=2.0)
+            P(nm("wb"), 1, lambda g, T, hh=hh: g.tensor.matmul(mr(T, 1), h16(T, 0), hh(T, 3), True, True), [t("b"), "H0", t("sg")], ["m1"], ["bm"])
+            V(nm("bfd"), CH, lambda g, T, hh=hh: g.vector.tensor_tensor(hh(T, 2), mr(T, 1), hh(T, 1), A.mult), ["m1", t("fd")], [t("bfd")], ["bm"])
+
+            def pw(g, T, hh=hh):
+                g.tensor.matmul(mr(T, 2), h16(T, 0), hh(T, 1), True, False)
+                g.tensor.matmul(mr(T, 2), h16(T, 2), hh(T, 2), False, True)
+                g.tensor.matmul(mr(T, 3), h16(T, 1), hh(T, 1), True, False)
+                return g.tensor.matmul(mr(T, 3), h16(T, 0), hh(T, 2), False, True)
+            P(nm("pw"), 4, pw, [t("fd"), t("bfd"), "H0", "H1", "H2"], ["m2", "m3"], ["bm"])
+            V(nm("wu"), 2 * CH, lambda g, T, gw=gw: g.vector.tensor_tensor(gw(T, 1, 2), mr(T, 2, 2), gw(T, 1, 2), A.add),
+              ["m2", "m3", t("gw1_"), t("gw2_")], [t("gw1_"), t("gw2_")], ["bm"])
+            if last:
+                o = 2 * CH * c
+                V(nm("w0"), CH, lambda g, T, gw=gw, o=o: g.vector.tensor_copy(T.ywb[:, o:o + 2 * CH:2], gw(T, 2)), [t("gw2_")], ["yw0%d" % c])
+                V(nm("w1"), 2 * CH, lambda g, T, gw=gw, o=o: g.vector.tensor_tensor(T.ywb[:, o + 1:o + 2 * CH:2], gw(T, 2), gw(T, 1), A.add),
+                  [t("gw1_"), t("gw2_")], ["yw1%d" % c])
+                op("Y", nm("yw"), 0.1, lambda g, T, o=o: g.sync.dma_start(T.yw[:, o:o + 2 * CH], T.ywb[:, o:o + 2 * CH]),
+                   R=["yw0%d" % c, "yw1%d" % c], W=["yw%d" % c], lat=2.0)
+            if c == NC - 1 and not last:
+                V(nm("fa"), 6, lambda g, T: g.vector.tensor_copy(T.accb[:], T.acc[:]), ["acc%d" % j for j in range(6)], ["accb"])
+
+                def ft(g, T):
+                    for j in range(6):
+                        r = g.tensor.matmul(T.bf[:, 448:449], mat(T, "ONE" if j < 3 else "nONE"), T.accb[:, j:j + 1], j == 0, j == 5)
+                    return r
+                P(nm("ft"), 6, ft, ["accb", "ONE", "nONE"], ["f7"], ["bf"])
+                V(nm("fi"), 1, lambda g, T: g.vector.tensor_copy(T.fi[:, 0:1], T.bf[:, 448:449]), ["f7"], ["fi"], ["bf"])
+                V(nm("fj"), 1, lambda g, T: g.vector.tensor_scalar(T.fj[:, 0:1], T.fi[:, 0:1], 31, None, A.bitwise_and), ["fi"], ["fj"])
+                V(nm("tA"), 1, lambda g, T: g.vector.tensor_scalar(col(T, "thA"), T.fj[:, 0:1], 16.0, col(T, "thm"), A.mult, A.add),
+                  ["fj", "c_thm"], ["c_thA"])
+    return ops
+
+
+def modulo(ops, per, wgt=None, send=2.5 + 1.1, res=0.01):
+    pat = [o for o in ops if o["name"].endswith(".2.0") and o["eng"] in "VSPN"]
+    key = {o["k"]: o["name"].split(".")[0] for o in pat}
+    succ = {k: [] for k in key}
+    for o in pat:
+        for d in o["deps"]:
+            if d in key:
+                succ[d].append(o["k"])
+    tail = {}
+    for o in reversed(pat):
+        k = o["k"]
+        tail[k] = o["cost"] + (send if key[k] == "kn" else 0.0) + max([tail[s] + WAKE for s in succ[k]] or [0.0])
+    for k in tail:
+        tail[k] += (wgt or {}).get(key[k], 0.0)
+    npred = {o["k"]: len([d for d in o["deps"] if d in key]) for o in pat}
+    ready = [k for k in key if npred[k] == 0]
+    use, tau, fin = [], {}, {}
+    cells = int(round(per / res))
+    eng = {}
+    bnk = {}
+    while ready:
+        k = max(ready, key=lambda x: (tail[x], -x))
+        ready.remove(k)
+        o = ops[k]
+        s = 0.0
+        for d in o["deps"]:
+            if d in key:
+                s = max(s, fin[d] + WAKE)
+        if o["eng"] == "N":
+            tau[k], fin[k] = 0.0, 0.0 if key[k] == "az" else (wgt or {}).get("AK", 0.6)
+        else:
+            c0 = int(math.ceil(s / res - 1e-6))
+            n = int(math.ceil(o["cost"] / res))
+            e = eng.setdefault(o["eng"], set())
+            bs = [bnk.setdefault(b, {}) for b in o["banks"]]
+            c = c0
+            while c < c0 + cells:
+                bad = None
+                for i in range(c, c + n):
+                    m = i % cells
+                    if m in e or any(b.get(m, o["eng"]) != o["eng"] for b in bs):
+                        bad = i
+                        break
+                if bad is None:
+                    break
+                c = bad + 1
+            for i in range(c, c + n):
+                e.add(i % cells)
+                for b in bs:
+                    b[i % cells] = o["eng"]
+            tau[k], fin[k] = c * res, (c + n) * res
+        for x in succ[k]:
+            npred[x] -= 1
+            if npred[x] == 0:
+                ready.append(x)
+    return {key[k]: v for k, v in tau.items()}, max(fin[k] for k in key if key[k] == "kn")
+
+
+def schedule(ops, tau=None, per=0.0):
+    n = len(ops)
+    succ = [[] for _ in range(n)]
+    for o in ops:
+        for d in o["deps"] | o["soft"]:
+            succ[d].append(o["k"])
+    tail = [0.0] * n
+    for k in range(n - 1, -1, -1):
+        o = ops[k]
+        tail[k] = o["cost"] + o["lat"] + max([tail[s] + WAKE for s in succ[k]] or [0.0])
+    for k in range(n):
+        nme = ops[k]["name"].split(".")
+        tail[k] += BIAS.get(nme[0], 0.0)
+        if tau and len(nme) == 3:
+            tail[k] = -(tau.get(nme[0], 0.0) + per * (NC * int(nme[1]) + int(nme[2])))
+    left = [len(o["deps"] | o["soft"]) for o in ops]
+    ready = [k for k in range(n) if left[k] == 0]
+    end = [None] * n
+    free, order = {}, {}
+    bank = {}
+    while ready:
+        cand = {}
+        for k in ready:
+            o = ops[k]
+            s = free.get(o["eng"], 0.0) if o["eng"] != "N" else 0.0
+            for d in o["deps"] | o["soft"]:
+                w = 0.0 if (ops[d]["eng"] == o["eng"] and d not in o["deps"]) else WAKE
+                s = max(s, end[d] + ops[d]["lat"] + w)
+            for b in o["banks"]:
+                for q, x in bank.get(b, {}).items():
+                    if q != o["eng"]:
+                        s = max(s, end[x] + WAKE)
+            cand.setdefault(o["eng"], []).append((s, k))
+        best = None
+        for q, l in cand.items():
+            s0 = min(l)[0]
+            s, k = max((x for x in l if x[0] <= s0 + AHEAD), key=lambda x: (tail[x[1]], -x[1]))
+            if best is None or s0 < best[0]:
+                best = (s0, s, k)
+        _, s, k = best
+        o = ops[k]
+        end[k] = s + o["cost"]
+        if o["eng"] != "N":
+            free[o["eng"]] = end[k]
+        order.setdefault(o["eng"], []).append(k)
+        o["start"] = s
+        for b in o["banks"]:
+            u = bank.setdefault(b, {})
+            for q, x in u.items():
+                if q != o["eng"]:
+                    o["soft"].add(x)
+            u[o["eng"]] = k
+        ready.remove(k)
+        for x in succ[k]:
+            left[x] -= 1
+            if left[x] == 0:
+                ready.append(x)
+    return order, end
+
+
+for _c in range(NC):
+    SCRATCH["vv%d" % _c] = ("sbuf", [128, CH], "float16")
+PLAN = {}
+
+
+def plan():
+    if "ops" not in PLAN:
+        ops = build()
+        order, end = schedule(ops, modulo(ops, PER)[0], PER)
+        glob = sorted((o["start"], o["k"]) for o in ops)
+        PLAN["ops"] = ops
+        PLAN["glob"] = [k for _, k in glob]
+        PLAN["end"] = end
+        cnt = {}
+        for q, l in order.items():
+            c = 0
+            for k in l:
+                o = ops[k]
+                if q in SEM and not (q == "G" and isinstance(o["fn"], tuple)):
+                    c += 1
+                o["cnt"] = c
+            cnt[q] = c
+        PLAN["order"], PLAN["cnt"] = order, cnt
+    return PLAN
+
+
+def rank_program(g, core, T, topo):
+    rank = T.rank_of(core)
+    if rank is None:
+        return
+    pl = plan()
+    ops, order = pl["ops"], pl["order"]
+    nxt = T.cores[(rank + 1) % len(T.cores)]
+    prv = T.cores[(rank - 1) % len(T.cores)]
+    rid, pid = topo.addr(nxt, core)
+    mask = topo.mask(core, nxt)
+    neng = len(topo.engines(core, nxt))
+    narr = len(topo.engines(prv, core))
+    que = {"V": g.vector, "S": g.scalar, "P": g.tensor, "G": g, "Y": g.sync}
+
+    for x, q, dst in (("gx", g.scalar, T.gxb[:]), ("rk", g.sync, T.rkb[:]), ("z0", g.sync, T.zin[:, 0:192]), ("wt", g.sync, T.wtb[:]),
+                      ("rt", g.sync, T.rtb[:]), ("sy", g.scalar, T.syb[:]), ("wr", g.sync, T.wrb[:]), ("th", g.sync, T.thb[:])):
+        q.dma_start(dst, T[x][:]).then_inc(T.sem["ld_" + x], 16)
+
+    know = {q: {} for q in que}
+    snap = {}
+    fin = [0]
+
+    def need(q, k, hard):
+        o = ops[k]
+        if o["eng"] == "N":
+            nme, v = o["sem"]
+            return nme, v if v else narr
+        if o["eng"] == q and not hard:
+            return None
+        return SEM[o["eng"]], o["cnt"]
+
+    for k in pl["glob"]:
+        o = ops[k]
+        q = o["eng"]
+        if q == "N":
+            s = {}
+            for d in o["deps"]:
+                pass
+            snap[k] = s
+            continue
+        req = {}
+        for d, hard in [(d, True) for d in o["deps"]] + [(d, False) for d in o["soft"]]:
+            if ops[d]["eng"] == "G" and isinstance(ops[d]["fn"], tuple):
+                continue
+            r = need(q, d, hard)
+            if r is None:
+                continue
+            req.setdefault(r[0], (0, None))
+            if r[1] > req[r[0]][0]:
+                req[r[0]] = (r[1], d)
+        kn = know[q]
+        for nme, (v, d) in sorted(req.items(), key=lambda x: -ops[x[1][1]].get("start", 0.0)):
+            if kn.get(nme, 0) >= v:
+                continue
+            que[q].wait_ge(T.sem[nme], v)
+            for a, b in snap[d].items():
+                if kn.get(a, 0) < b:
+                    kn[a] = b
+            kn[nme] = max(kn.get(nme, 0), v)
+        if isinstance(o["fn"], tuple):
+            _, kind, e, c, base = o["fn"]
+            src, dst = (T.zout, T.zin) if kind == "z" else (T.kout, T.kin)
+            b2 = 192 * (e + 1) + CH * c
+            g.remote_dma(dst[:, b2:b2 + CH], src[:, base:base + CH], T.sem["a%s%d_%d" % (kind, e + 1, c)], T.sem.loc, pid, rid, mask)
+            fin[0] += neng
+        else:
+            ins = o["fn"](g, T)
+            if q == "Y":
+                ins.then_inc(T.sem.fin, 16)
+            else:
+                ins.then_inc(T.sem[SEM[q]], 1)
+        snap[k] = dict(kn)
+    g.wait_ge(T.sem.loc, fin[0])
+    g.wait_ge(T.sem.fin, 16 * len(order["Y"]))
+    for q, s in SEM.items():
+        g.wait_ge(T.sem[s], pl["cnt"][q])
+    for o in ops:
+        if o["eng"] == "N":
+            nme, v = o["sem"]
+            g.wait_ge(T.sem[nme], v if v else narr)

@@ -12,11 +12,15 @@ GAM = 1.5
 CY = 0.00083
 PC = 0.00042
 AHEAD = 0.0
-PER = 5.3
-BIAS = {}
+PER = 12.0
+BIAS = {'k32': 0.6, 'T1': -2.1, 'cs0': -2.3, 'pw': 12.0, 'cl0': -14.0, 'dg3': -3.1, 'sk': 13.1, 'po': 3.3, 'ko': -1.0, 'sz': -1.1,
+        'tA': 3.6, 'sgea1': 2.8, 'm1': 3.2, 'fa': 5.6, 'sgeb0': 0.6, 'w1': -11.1, 'mkeb': 5.0, 'r5': 1.6, 'Eeb': -0.6, 'ab3': 2.7,
+        'bd': 1.3, 'cl1': 0.5, 'nz': -1.6, 'sg': 1.8, 'sgea0': 0.5, 'ph': 3.2, 'R2': 13.8, 'dp': 5.8, 'ab0': -0.4, 'w0': -0.5,
+        'fc': -6.0, 'bb': 11.2, 'mkea': 0.9, 'fj': 2.2, 'R3': 1.7, 'wu': 1.2, 'bfd': 0.6, 'vs': 1.1, 'ab2': -0.6, 'cs1': -2.4,
+        'thr': 0.4, 't2': 0.7, 't4': 0.4, 't3': 0.9, 'hs': -0.2, 'za': -0.2, 'r3': 0.1, 'wb': 0.1, 'fd': -0.1, 'nu': -0.1}
 XP = 4
 SCB = True
-WAKE = 0.06
+WAKE = 0.17
 
 SCRATCH = {
     "gxb": ("sbuf", [128, 2048], "bfloat16"), "syb": ("sbuf", [128, 2048], "bfloat16"),
@@ -30,11 +34,12 @@ SCRATCH = {
     "tq0": ("sbuf", [128, 128], "float32"),
     "cols": ("sbuf", [128, 16], "float32"), "rmn": ("sbuf", [128, 16], "float32"), "rm1": ("sbuf", [128, 16], "float32"),
     "w37": ("sbuf", [128, 1], "int32"), "w37l": ("sbuf", [128, 1], "int32"),
-    "mats": ("sbuf", [128, 24 * 128], "bfloat16"), "m16": ("sbuf", [128, 3 * 128], "float16"),
+    "mats": ("sbuf", [128, 24 * 128], "bfloat16"), "m16": ("sbuf", [128, 4 * 128], "float16"),
+    "on16": ("sbuf", [128, CH], "float16"),
     "bc": ("sbuf", [128, 2048], "bfloat16"), "bv": ("sbuf", [128, 2048], "float16"),
     "bk": ("sbuf", [128, 2048], "bfloat16"), "tp": ("sbuf", [128, 2048], "bfloat16"),
     "rst": ("sbuf", [128, 512], "bfloat16"),
-    "acc": ("sbuf", [128, 6], "float32"), "accb": ("sbuf", [128, 6], "bfloat16"),
+    "acc": ("sbuf", [128, NC], "float32"), "accb": ("sbuf", [128, NC], "bfloat16"),
     "fi": ("sbuf", [128, 1], "int32"), "fj": ("sbuf", [128, 1], "int32"),
     "ea0": ("psum", [128, 512], "float32"), "eb0": ("psum", [128, 512], "float32"),
     "ea1": ("psum", [128, 512], "float32"), "eb1": ("psum", [128, 512], "float32"),
@@ -44,7 +49,7 @@ SCRATCH = {
 for _c in range(NC):
     for _n, _w, _d in (("gw", 4 * CH, "float16"), ("ko", CH, "uint16"), ("so", CH, "uint16"), ("xg", FULL, "bfloat16"),
                        ("dg", FULL, "bfloat16"), ("ab", FULL, "bfloat16"), ("cc", FULL, "float16"),
-                       ("ii", 4 * CH, "int32"), ("tt", 4 * CH, "int32"), ("hh", 4 * CH, "float16"), ("bd", 2 * CH, "float16"),
+                       ("ii", 4 * CH, "int32"), ("tt", 9 * CH, "int32"), ("hh", 4 * CH, "float16"), ("bd", CH, "float16"), ("thr", CH, "float32"),
                        ("sm", 12 * CH, "bfloat16")):
         SCRATCH["%s%d" % (_n, _c)] = ("sbuf", [128, _w], _d)
     for _n in ("ha", "hb", "ra", "rb", "eb"):
@@ -54,8 +59,8 @@ LOADS = ["rk", "z0", "wt", "gx", "rt", "wr", "th", "sy"]
 SEMAPHORES = ["sv", "ss", "sp", "sg", "loc", "fin"] + ["ld_" + x for x in LOADS] + \
     ["az%d_%d" % (e, c) for e in range(1, LE) for c in range(NC)] + ["ak%d_%d" % (e, c) for e in range(1, LE) for c in range(NC)]
 
-MAT = ["BLK", "I", "nI", "I16", "I256", "n32I", "GE", "U", "L", "LS", "US", "nU", "hU", "ONE", "nONE", "TQ", "W", "WH", "WL",
-       "I4", "IT", "x1", "x2"]
+MAT = ["BLK", "I", "nI", "I128", "I512", "n128I", "GE", "L2", "U", "L", "LP", "UM", "nU", "U2", "DK", "ONE", "nONE", "TQ", "W", "WH", "WL",
+       "I4", "IT", "x1"]
 COL = ["p", "k", "g", "b2", "b3", "pos", "kc", "thm", "thA", "wh", "wl"]
 SEM = {"V": "sv", "S": "ss", "P": "sp", "G": "sg"}
 
@@ -115,7 +120,8 @@ def build():
         V(name, 128, lambda g, T: g.vector.tensor_scalar(mat(T, name), T.mi[:], col(T, "p"), float(s), A.is_equal, A.mult),
           ["mi", "c_p"], [name])
     diag("I", 1.0)
-    for j, s in enumerate((1.0, -1.0, -2.0)):
+    V("on16", CH, lambda g, T: g.vector.tensor_scalar(T.on16[:], T.mi[:, 0:CH], 0.0, 1.0, A.mult, A.add), ["mi"], ["on16"])
+    for j, s in enumerate((1.0, -1.0, -2.0, 32.0)):
         V("H%d" % j, 128, lambda g, T, j=j, s=s: g.vector.tensor_scalar(h16(T, j), T.mi[:], col(T, "p"), s, A.is_equal, A.mult),
           ["mi", "c_p"], ["H%d" % j])
     V("w37", 1, lambda g, T: g.vector.tensor_scalar(T.w37[:, 0:1], T.wtb[:, 0:1], 37.0, None, A.mult), ["in_wt"], ["w37"])
@@ -142,21 +148,21 @@ def build():
         P("trs%d" % q, 8, trs, ["IT"] + ["bc%d" % k for k in range(4 * q, 4 * q + 4)], ["p_" + b], [b])
         S("bk%d" % q, 512, lambda g, T, q=q: g.scalar.activation(T.bk[:, 512 * q:512 * q + 512], (T.ta if q % 2 == 0 else T.tb)[:], AF.Copy),
           ["p_" + b], ["bk%d" % q], [b])
-    diag("I16", 16.0)
-    diag("I256", 256.0)
-    diag("n32I", -32.0)
+    diag("I128", 128.0)
+    diag("I512", 512.0)
+    diag("n128I", -128.0)
     V("GE0", 128, lambda g, T: g.vector.tensor_scalar(mat(T, "x1"), T.mi[:], col(T, "p"), None, A.is_le), ["mi", "c_p"], ["x1"])
     tt = lambda name, a, b, o: V(name, 256, lambda g, T: g.vector.tensor_tensor(mat(T, name), mat(T, a), mat(T, b), o), [a, b], [name])
     tt("GE", "x1", "BLK", A.mult)
     tt("U", "GE", "I", A.subtract)
     tt("L", "BLK", "GE", A.subtract)
-    V("x2", 64, lambda g, T: g.vector.tensor_scalar(mat(T, "x2"), mat(T, "L"), 0.5, None, A.mult), ["L"], ["x2"])
-    tt("LS", "x2", "n32I", A.subtract)
-    tt("US", "U", "I16", A.subtract)
-    V("nU", 64, lambda g, T: g.vector.tensor_scalar(mat(T, "nU"), mat(T, "U"), -1.0, None, A.mult), ["U"], ["nU"])
-    V("hU", 64, lambda g, T: g.vector.tensor_scalar(mat(T, "hU"), mat(T, "U"), -0.5, None, A.mult), ["U"], ["hU"])
-    for n, a, b in (("b2", 0.5, -32.0), ("b3", 1.0, -16.0), ("pos", -1.0, 16.0), ("kc", 2048.0, -30720.0)):
+    for n, x, s in (("L2", "L", 2.0), ("nU", "U", -2.0), ("U2", "U", 2.0)):
+        V(n, 64, lambda g, T, n=n, x=x, s=s: g.vector.tensor_scalar(mat(T, n), mat(T, x), s, None, A.mult), [x], [n])
+    tt("LP", "L2", "I128", A.add)
+    tt("UM", "U2", "I128", A.subtract)
+    for n, a, b in (("b3", 2.0, 1.0), ("pos", -2.0, 31.0), ("kc", 2048.0, -30720.0)):
         V("c_" + n, 1, lambda g, T, n=n, a=a, b=b: g.vector.tensor_scalar(col(T, n), col(T, "k"), a, b, A.mult, A.add), ["c_k"], ["c_" + n])
+    V("DK", 64, lambda g, T: g.vector.tensor_scalar(mat(T, "DK"), mat(T, "I"), col(T, "pos"), None, A.mult), ["I", "c_pos"], ["DK"])
     V("thm", 1, lambda g, T: g.vector.tensor_scalar(col(T, "thm"), T.thb[:, 0:1], -0.5, None, A.add), ["in_th"], ["c_thm"])
     V("ONE", 64, lambda g, T: g.vector.memset(mat(T, "ONE"), 1.0), [], ["ONE"])
     V("nONE", 64, lambda g, T: g.vector.memset(mat(T, "nONE"), -1.0), [], ["nONE"])
@@ -185,12 +191,11 @@ def build():
         sl = slice(CH * c, CH * c + CH)
         V("k0_%d" % c, CH, lambda g, T, sl=sl: g.vector.tensor_copy(T.kin[:, sl], T.rkb[:, sl]), ["in_rk"], ["kin0_%d" % c])
         ev, od = slice(2 * CH * c, 2 * CH * c + 2 * CH, 2), slice(2 * CH * c + 1, 2 * CH * c + 2 * CH, 2)
-        for src, base, dif in (("rt", 3, 0), ("wr", 2, 1)):
-            V("%sb%d" % (src, c), CH, lambda g, T, c=c, src=src, base=base, ev=ev:
-              g.vector.tensor_copy(T["gw%d" % c][:, CH * base:CH * base + CH], T[src + "b"][:, ev]), ["in_" + src], ["gw%d_%d" % (base, c)])
-            V("%sd%d" % (src, c), 2 * CH, lambda g, T, c=c, src=src, dif=dif, ev=ev, od=od:
-              g.vector.tensor_tensor(T["gw%d" % c][:, CH * dif:CH * dif + CH], T[src + "b"][:, od], T[src + "b"][:, ev], A.subtract),
-              ["in_" + src], ["gw%d_%d" % (dif, c)])
+        for src, base, cut in (("rt", 0, ev), ("rt", 1, od), ("wr", 3, ev)):
+            V("%s%d_%d" % (src, base, c), CH, lambda g, T, c=c, src=src, base=base, cut=cut:
+              g.vector.tensor_copy(T["gw%d" % c][:, CH * base:CH * base + CH], T[src + "b"][:, cut]), ["in_" + src], ["gw%d_%d" % (base, c)])
+        V("wrd%d" % c, 2 * CH, lambda g, T, c=c, ev=ev, od=od: g.vector.tensor_tensor(
+            T["gw%d" % c][:, CH * 2:CH * 3], T.wrb[:, od], T.wrb[:, ev], A.subtract), ["in_wr"], ["gw2_%d" % c])
 
     fr = lambda T, j, n=1: T.bf[:, 64 * j:64 * j + 64 * n]
     mr = lambda T, j, n=1: T.bm[:, 64 * j:64 * j + 64 * n]
@@ -205,7 +210,7 @@ def build():
             t = lambda x, c=c: "%s%d" % (x, c)
             sm = lambda T, j, c=c: T["sm%d" % c][:, CH * j:CH * j + CH]
             ii = lambda T, j, c=c: T["ii%d" % c][:, CH * j:CH * j + CH]
-            tb = lambda T, j, c=c: T["tt%d" % c][:, CH * j:CH * j + CH]
+            tb = lambda T, j, m=1, c=c: T["tt%d" % c][:, CH * j:CH * j + CH * m]
             hh = lambda T, j, c=c: T["hh%d" % c][:, CH * j:CH * j + CH]
             gw = lambda T, j, m=1, c=c: T["gw%d" % c][:, CH * j:CH * j + CH * m]
             nm = lambda x, e=e, c=c: "%s.%d.%d" % (x, e, c)
@@ -227,34 +232,34 @@ def build():
               [t("ii2")], [t("ii3")])
             V(nm("r5"), CH, lambda g, T, ii=ii, hh=hh: g.vector.tensor_copy(hh(T, 3), ii(T, 3)), [t("ii3")], [t("b")])
 
-            def fb(g, T, hh=hh):
-                g.tensor.matmul(fr(T, 1), h16(T, 0), hh(T, 3), True, True)
-                return g.tensor.matmul(fr(T, 2), h16(T, 0), hh(T, 3), True, True)
-            P(nm("fb"), 2, fb, [t("b"), "H0"], ["f1"], ["bf"])
-            V(nm("bd"), 2 * CH, lambda g, T, t=t, gw=gw: g.vector.tensor_tensor(T[t("bd")][:], gw(T, 0, 2), fr(T, 1, 2), A.mult),
-              ["f1", t("gw0_"), t("gw1_")], [t("bd")], ["bf"])
-
-            def rq(g, T, t=t, gw=gw, zin=zin):
-                i = h16(T, 0)
-                g.tensor.matmul(fr(T, 3), i, gw(T, 3), True, False)
-                g.tensor.matmul(fr(T, 3), i, T[t("bd")][:, 0:CH], False, True)
-                g.tensor.matmul(fr(T, 5), mat(T, "WH"), zin(T), True, False)
-                g.tensor.matmul(fr(T, 5), mat(T, "WL"), zin(T), False, False)
-                g.tensor.matmul(fr(T, 5), i, gw(T, 3), False, False)
-                r = g.tensor.matmul(fr(T, 5), i, T[t("bd")][:, 0:CH], False, True)
+            def k32(g, T, kin=kin):
+                for j in (3, 4):
+                    g.tensor.matmul(fr(T, j), h16(T, 3), T.on16[:], True, False)
+                    r = g.tensor.matmul(fr(T, j), h16(T, 0), kin(T), False, True)
                 return r
+            P(nm("k32"), 4, k32, [K_, "H0", "H3", "on16"], ["f3"], ["bf"])
+
+            def u37(g, T, zin=zin):
+                g.tensor.matmul(fr(T, 5), mat(T, "WH"), zin(T), True, False)
+                return g.tensor.matmul(fr(T, 5), mat(T, "WL"), zin(T), False, True)
+            P(nm("u37"), 2, u37, [Z_, "WH", "WL"], ["f5"], ["bf"])
+            V(nm("t1"), 2 * CH, lambda g, T, tb=tb, gw=gw: g.vector.tensor_tensor(tb(T, 0, 2), fr(T, 3, 2), gw(T, 0, 2), A.mult),
+              ["f3", t("gw0_"), t("gw1_")], [t("t0")], ["bf"])
+            V(nm("t2"), 2 * CH, lambda g, T, tb=tb: g.vector.tensor_scalar(tb(T, 2, 2), tb(T, 0, 2), 5, None, A.arith_shift_right), [t("t0")], [t("t1")])
+            V(nm("dp"), 2 * CH, lambda g, T, tb=tb: g.vector.tensor_tensor(tb(T, 4), tb(T, 3), tb(T, 2), A.subtract), [t("t1")], [t("dp")])
+            V(nm("pu"), CH, lambda g, T, tb=tb: g.vector.tensor_tensor(tb(T, 5), fr(T, 5), tb(T, 2), A.add), [t("t1"), "f5"], [t("pu")], ["bf"])
+            V(nm("bp"), 2 * CH, lambda g, T, tb=tb, ii=ii: g.vector.tensor_tensor(tb(T, 6), tb(T, 4), ii(T, 3), A.mult), [t("dp"), t("ii3")], [t("bp")])
+            V(nm("t3"), 2 * CH, lambda g, T, tb=tb: g.vector.tensor_tensor(tb(T, 7), tb(T, 6), tb(T, 5), A.add), [t("bp"), t("pu")], [t("t2")])
+            V(nm("t4"), CH, lambda g, T, tb=tb: g.vector.tensor_scalar(tb(T, 8), tb(T, 7), 2047, None, A.bitwise_and), [t("t2")], [t("t3")])
+            V(nm("so"), CH, lambda g, T, t=t, tb=tb: g.vector.tensor_copy(T[t("so")][:], tb(T, 8)), [t("t3")], [t("so")])
+            P(nm("fb"), 1, lambda g, T, hh=hh: g.tensor.matmul(fr(T, 1), h16(T, 0), hh(T, 3), True, True), [t("b"), "H0"], ["f1"], ["bf"])
+            V(nm("bd"), CH, lambda g, T, t=t, gw=gw: g.vector.tensor_tensor(T[t("bd")][:], fr(T, 1), gw(T, 2), A.mult),
+              ["f1", t("gw2_")], [t("bd")], ["bf"])
 
             def od(g, T, t=t, gw=gw, kin=kin):
-                i = h16(T, 0)
-                g.tensor.matmul(fr(T, 4), i, gw(T, 2), True, False)
-                g.tensor.matmul(fr(T, 4), h16(T, 1), kin(T), False, False)
-                return g.tensor.matmul(fr(T, 4), i, T[t("bd")][:, CH:2 * CH], False, True)
-            P(nm("rq"), 6, rq, [t("bd"), t("gw3_"), Z_, "H0", "WH", "WL"], ["f3", "f5"], ["bf"])
-            V(nm("t1"), CH, lambda g, T, tb=tb, kin=kin: g.vector.tensor_tensor(tb(T, 0), fr(T, 3), kin(T), A.mult), ["f3", K_], [t("t0")], ["bf"])
-            V(nm("t2"), CH, lambda g, T, tb=tb: g.vector.tensor_scalar(tb(T, 1), tb(T, 0), 5, None, A.arith_shift_right), [t("t0")], [t("t1")])
-            V(nm("t3"), CH, lambda g, T, tb=tb: g.vector.tensor_tensor(tb(T, 2), fr(T, 5), tb(T, 1), A.add), [t("t1"), "f5"], [t("t2")], ["bf"])
-            V(nm("t4"), CH, lambda g, T, tb=tb: g.vector.tensor_scalar(tb(T, 3), tb(T, 2), 2047, None, A.bitwise_and), [t("t2")], [t("t3")])
-            V(nm("so"), CH, lambda g, T, t=t, tb=tb: g.vector.tensor_copy(T[t("so")][:], tb(T, 3)), [t("t3")], [t("so")])
+                g.tensor.matmul(mr(T, 4), h16(T, 0), gw(T, 3), True, False)
+                g.tensor.matmul(mr(T, 4), h16(T, 1), kin(T), False, False)
+                return g.tensor.matmul(mr(T, 4), h16(T, 0), T[t("bd")][:], False, True)
             for q in range(XP):
                 a, b = FULL // XP * q, FULL // XP * (q + 1)
                 V(nm("dg%d" % q), 0, lambda g, T, t=t, q=q, a=a, b=b: g.vector.tensor_tensor(
@@ -297,50 +302,48 @@ def build():
                 return r
             P(nm("hs"), 16, hsum, [t(x) + "_%d" % a for x in ("ha", "hb") for a in range(2)] + ["bk%d" % q for q in range(4)], ["m0"], ["bm"])
             th = "c_thm" if e == 0 else "c_thA"
-            S(nm("hr"), CH, lambda g, T, sm=sm: g.scalar.activation(sm(T, 0), mr(T, 0), AF.Relu), ["m0"], [t("hr")], ["bm"])
-            S(nm("sp"), CH, lambda g, T, sm=sm, e=e, c=c: g.scalar.activation(
-                sm(T, 1), fr(T, 6), AF.Sign, scale=-1.0, bias=col(T, "thm" if e == 0 else "thA"), accum_out=T.acc[:, c:c + 1]),
-              ["f6", th], [t("sp"), "acc%d" % c], ["bf"])
-
-            def h2(g, T, sm=sm):
-                g.tensor.matmul(mr(T, 1), mat(T, "I"), sm(T, 0), True, False)
-                return g.tensor.matmul(mr(T, 1), mat(T, "I16"), sm(T, 1), False, True)
-            P(nm("h2"), 2, h2, [t("hr"), t("sp"), "I", "I16"], ["m1"], ["bm"])
-            S(nm("hp"), CH, lambda g, T, sm=sm: g.scalar.activation(sm(T, 2), mr(T, 1), AF.Relu, bias=-16.0), ["m1"], [t("hp")], ["bm"])
+            tcol = "thm" if e == 0 else "thA"
+            V(nm("thr"), CH, lambda g, T, t=t, tcol=tcol: g.vector.tensor_scalar(T[t("thr")][:], mr(T, 0), 1.0, col(T, tcol), A.is_gt, A.mult),
+              ["m0", th], [t("thr")], ["bm"])
+            V(nm("ph"), CH, lambda g, T, t=t, sm=sm: g.vector.tensor_tensor(sm(T, 2), fr(T, 6), T[t("thr")][:], A.is_lt),
+              ["f6", t("thr")], [t("ph")], ["bf"])
+            V(nm("pl"), CH, lambda g, T, sm=sm, tcol=tcol: g.vector.tensor_scalar(sm(T, 1), fr(T, 6), col(T, tcol), None, A.is_lt),
+              ["f6", th], [t("pl")], ["bf"])
 
             def vs(g, T, sm=sm):
-                g.tensor.matmul(mr(T, 2), mat(T, "GE"), sm(T, 2), True, False)
-                return g.tensor.matmul(mr(T, 2), mat(T, "I256"), sm(T, 1), False, True)
-            P(nm("vs"), 2, vs, [t("hp"), t("sp"), "GE", "I256"], ["m2"], ["bm"])
-            S(nm("sg"), CH, lambda g, T, sm=sm, c=c: g.scalar.activation(sm(T, 3), mr(T, 2), AF.Sign, bias=-256.0,
-                                                                        accum_out=T.acc[:, 3 + c:4 + c]),
-              ["m2"], [t("sg"), "acc%d" % (3 + c)], ["bm"])
+                for o in (fr(T, 2), mr(T, 3)):
+                    g.tensor.matmul(o, mat(T, "GE"), sm(T, 2), True, False)
+                    r = g.tensor.matmul(o, mat(T, "I512"), sm(T, 1), False, True)
+                return r
+            P(nm("vs"), 4, vs, [t("ph"), t("pl"), "GE", "I512"], ["f2", "m3"], ["bf", "bm"])
+            V(nm("nu"), CH, lambda g, T, sm=sm: g.vector.tensor_scalar(sm(T, 7), fr(T, 2), 512.5, None, A.is_lt), ["f2"], [t("nu")], ["bf"])
+            V(nm("fl"), CH, lambda g, T, sm=sm: g.vector.tensor_scalar(sm(T, 11), fr(T, 2), 512.0, None, A.is_equal), ["f2"], [t("fl")], ["bf"])
+            S(nm("sg"), CH, lambda g, T, sm=sm: g.scalar.activation(sm(T, 3), mr(T, 3), AF.Sign, bias=-512.0), ["m3"], [t("sg")], ["bm"])
+            S(nm("fc"), CH, lambda g, T, sm=sm, c=c: g.scalar.activation(sm(T, 0), sm(T, 11), AF.Copy, accum_out=T.acc[:, c:c + 1]),
+              [t("fl")], [t("fcs"), "acc%d" % c])
 
-            def bb(g, T, sm=sm, hh=hh, kin=kin):
-                s, p = sm(T, 3), sm(T, 1)
-                g.tensor.matmul(mr(T, 3), mat(T, "LS"), p, True, False)
-                g.tensor.matmul(mr(T, 3), mat(T, "n32I"), s, False, True)
-                g.tensor.matmul(mr(T, 4), mat(T, "US"), p, True, False)
-                return g.tensor.matmul(mr(T, 4), mat(T, "nU"), s, False, True)
-            P(nm("bb"), 4, bb, [t("sg"), t("sp"), "LS", "n32I", "US", "nU"], ["m3", "m4"], ["bm"])
-            P(nm("od"), 3, od, [t("bd"), t("gw2_"), K_, "H0", "H1", t("sp")], ["f4"], ["bf"])
-            P(nm("kp"), 1, lambda g, T, kin=kin: g.tensor.matmul(mr(T, 5), h16(T, 0), kin(T), True, True), [K_, "H0", t("sg")], ["m5"], ["bm"])
-            S(nm("f0"), CH, lambda g, T, sm=sm: g.scalar.activation(sm(T, 10), sm(T, 3), AF.Abs), [t("sg")], [t("fa")])
-            S(nm("f1"), CH, lambda g, T, sm=sm: g.scalar.activation(sm(T, 11), sm(T, 10), AF.Copy, scale=-1.0, bias=1.0), [t("fa")], [t("fl")])
-            S(nm("R2"), CH, lambda g, T, sm=sm: g.scalar.activation(sm(T, 4), mr(T, 3), AF.Relu, bias=col(T, "b2")), ["m3", "c_b2"], [t("R2")], ["bm"])
-            S(nm("R3"), CH, lambda g, T, sm=sm: g.scalar.activation(sm(T, 5), mr(T, 4), AF.Relu, bias=col(T, "b3")), ["m4", "c_b3"], [t("R3")], ["bm"])
-            V(nm("fd"), CH, lambda g, T, hh=hh, sm=sm: g.vector.tensor_tensor(hh(T, 1), fr(T, 4), sm(T, 11), A.mult), ["f4", t("fl")], [t("fd")], ["bf"])
-            V(nm("v"), CH, lambda g, T, t=t, hh=hh: g.vector.tensor_tensor(T[t("vv")][:], mr(T, 5), hh(T, 1), A.add), ["m5", t("fd")], [t("v")], ["bm"])
+            def bb(g, T, sm=sm):
+                g.tensor.matmul(mr(T, 1), mat(T, "LP"), sm(T, 1), True, True)
+                return g.tensor.matmul(mr(T, 2), mat(T, "UM"), sm(T, 1), True, True)
+            P(nm("bb"), 2, bb, [t("pl"), "LP", "UM"], ["m1", "m2"], ["bm"])
+            S(nm("R2"), CH, lambda g, T, sm=sm: g.scalar.activation(sm(T, 4), mr(T, 1), AF.Relu, bias=-127.0), ["m1"], [t("R2")], ["bm"])
+            S(nm("R3"), CH, lambda g, T, sm=sm: g.scalar.activation(sm(T, 5), mr(T, 2), AF.Relu, bias=col(T, "b3")), ["m2", "c_b3"], [t("R3")], ["bm"])
 
             def po(g, T, sm=sm):
-                g.tensor.matmul(mr(T, 6), mat(T, "U"), sm(T, 3), True, False)
-                g.tensor.matmul(mr(T, 6), mat(T, "hU"), sm(T, 1), False, False)
+                g.tensor.matmul(mr(T, 6), mat(T, "I128"), sm(T, 1), True, False)
                 g.tensor.matmul(mr(T, 6), mat(T, "I"), sm(T, 4), False, False)
-                return g.tensor.matmul(mr(T, 6), mat(T, "I"), sm(T, 5), False, True)
-            P(nm("po"), 4, po, [t("sg"), t("sp"), t("R2"), t("R3"), "U", "hU", "I"], ["m6"], ["bm"])
-            S(nm("nu"), CH, lambda g, T, sm=sm: g.scalar.activation(sm(T, 7), sm(T, 3), AF.Copy, scale=-1.0, bias=1.0), [t("sg")], [t("nu")])
-            S(nm("pp"), CH, lambda g, T, sm=sm: g.scalar.activation(sm(T, 6), mr(T, 6), AF.Identity, scale=2.0, bias=col(T, "pos")),
-              ["m6", "c_pos"], [t("pp")], ["bm"])
+                g.tensor.matmul(mr(T, 6), mat(T, "I"), sm(T, 5), False, False)
+                g.tensor.matmul(mr(T, 6), mat(T, "n128I"), sm(T, 3), False, True)
+                g.tensor.matmul(mr(T, 7), mat(T, "DK"), mat(T, "ONE")[:, 0:CH], True, False)
+                g.tensor.matmul(mr(T, 7), mat(T, "nU"), sm(T, 1), False, False)
+                return g.tensor.matmul(mr(T, 7), mat(T, "U2"), sm(T, 3), False, True)
+            P(nm("po"), 7, po, [t("sg"), t("pl"), t("R2"), t("R3"), "U2", "nU", "I", "I128", "n128I", "DK", "ONE"], ["m6", "m7"], ["bm"])
+            S(nm("ry"), CH, lambda g, T, sm=sm: g.scalar.activation(sm(T, 10), mr(T, 6), AF.Relu, bias=-128.0), ["m6"], [t("ry")], ["bm"])
+            V(nm("pp"), CH, lambda g, T, sm=sm: g.vector.tensor_tensor(sm(T, 6), mr(T, 7), sm(T, 10), A.max), ["m7", t("ry")], [t("pp")], ["bm"])
+            P(nm("od"), 3, od, [t("bd"), t("gw3_"), K_, "H0", "H1", t("xg") + "_0"], ["m4"], ["bm"])
+            P(nm("kp"), 1, lambda g, T, kin=kin: g.tensor.matmul(mr(T, 5), h16(T, 0), kin(T), True, True), [K_, "H0", t("xg") + "_0"], ["m5"], ["bm"])
+            V(nm("fd"), CH, lambda g, T, hh=hh, sm=sm: g.vector.tensor_tensor(hh(T, 1), mr(T, 4), sm(T, 11), A.mult), ["m4", t("fl")], [t("fd")], ["bm"])
+            V(nm("v"), CH, lambda g, T, t=t, hh=hh: g.vector.tensor_tensor(T[t("vv")][:], mr(T, 5), hh(T, 1), A.add), ["m5", t("fd")], [t("v")], ["bm"])
             for bank, k0 in EB:
                 def mk(g, T, bank=bank, k0=k0, sm=sm):
                     for kk in range(8):
@@ -359,10 +362,10 @@ def build():
             else:
                 V(nm("scb"), 512, lambda g, T, t=t, bB=bB: g.vector.tensor_tensor_scan(T[t("rb")][:], T.rst[:], T[bB][:], 0.0, A.mult, A.max),
                   ["p_" + bB, "rst"], [t("rb")], [bB])
-            P(nm("nz"), 1, lambda g, T, zin=zin: g.tensor.matmul(mr(T, 4), mat(T, "nI"), zin(T), True, True), [Z_, "nI", t("R3")], ["m4"], ["bm"])
+            P(nm("nz"), 1, lambda g, T, zin=zin: g.tensor.matmul(mr(T, 0), mat(T, "nI"), zin(T), True, True), [Z_, "nI"], ["m0"], ["bm"])
             V(nm("m1"), 2 * CH, lambda g, T, t=t, sm=sm: g.vector.tensor_tensor(sm(T, 8), T[t("ra")][:, 7::8], T[t("rb")][:, 7::8], A.max),
               [t("ra") + "_0", t("ra") + "_1", t("rb")], [t("mx")])
-            V(nm("m2"), CH, lambda g, T, sm=sm: g.vector.tensor_tensor(sm(T, 9), mr(T, 4), sm(T, 8), A.add), [t("mx"), "m4"], [t("my")], ["bm"])
+            V(nm("m2"), CH, lambda g, T, sm=sm: g.vector.tensor_tensor(sm(T, 9), mr(T, 0), sm(T, 8), A.add), [t("mx"), "m0"], [t("my")], ["bm"])
             last = e == LE - 1
             S(nm("za"), CH, lambda g, T, sm=sm, base=base: g.scalar.activation(T.zout[:, base:base + CH], sm(T, 9), AF.Abs),
               [t("my")], ["zout%d_%d" % (e, c)])
@@ -371,62 +374,59 @@ def build():
             else:
                 op("Y", nm("yz"), 0.1, lambda g, T, base=base, c=c: g.sync.dma_start(T.yz[:, CH * c:CH * c + CH], T.zout[:, base:base + CH]),
                    R=["zout%d_%d" % (e, c)], W=["yz%d" % c], lat=2.0)
-            for h in range(4):
-                bank, lo = ("ta", "tb")[h % 2], 256 * (h // 2)
-
-                def tk(g, T, h=h, bank=bank, lo=lo, sm=sm, t=t):
-                    for kk in range(4):
-                        k = 4 * h + kk
-                        o = T[bank][:, lo + CH * kk:lo + CH * kk + CH]
+            for h, bank in enumerate(("ta", "tb")):
+                def tk(g, T, h=h, bank=bank, sm=sm, t=t):
+                    for kk in range(8):
+                        k = 8 * h + kk
+                        o = T[bank][:, CH * kk:CH * kk + CH]
                         g.tensor.matmul(o, T.tp[:, 128 * k:128 * k + 128], sm(T, 6), True, False)
                         r = g.tensor.matmul(o, T.bv[:, 128 * k:128 * k + 128], T[t("vv")][:], False, True)
                     return r
-                P(nm("T%d" % h), 8, tk, [t("pp"), t("v"), "tp%d" % h] + ["bv%d" % k for k in range(4 * h, 4 * h + 4)],
-                  ["p_%s%d" % (bank, h // 2)], [bank])
-                V(nm("cl%d" % h), 256, lambda g, T, bank=bank, lo=lo, h=h, t=t: g.vector.tensor_scalar(
-                    T[t("cc")][:, 256 * h:256 * h + 256], T[bank][:, lo:lo + 256], 0.0, 2048.0, A.max, A.min),
-                  ["p_%s%d" % (bank, h // 2)], [t("cc") + "_%d" % h], [bank])
-
-            def cs(g, T, t=t):
-                for k in range(16):
-                    r = g.tensor.matmul(mr(T, 7), h16(T, 0), T[t("cc")][:, CH * k:CH * k + CH], k == 0, k == 15)
-                return r
-            P(nm("cs"), 16, cs, [t("cc") + "_%d" % h for h in range(4)] + ["H0"], ["m7"], ["bm"])
+                P(nm("T%d" % h), 16, tk, [t("pp"), t("v"), "tp%d" % (2 * h), "tp%d" % (2 * h + 1)] + ["bv%d" % k for k in range(8 * h, 8 * h + 8)],
+                  ["p_" + bank], [bank])
+                V(nm("cl%d" % h), 512, lambda g, T, bank=bank, h=h, t=t: g.vector.tensor_scalar(
+                    T[t("cc")][:, 512 * h:512 * h + 512], T[bank][:], 0.0, 2048.0, A.max, A.min), ["p_" + bank], [t("cc") + "_%d" % h], [bank])
+            for h in range(2):
+                def cs(g, T, t=t, h=h):
+                    for k in range(8 * h, 8 * h + 8):
+                        r = g.tensor.matmul(T.ta[:, 0:CH], h16(T, 0), T[t("cc")][:, CH * k:CH * k + CH], k == 0, k == 15)
+                    return r
+                P(nm("cs%d" % h), 8, cs, [t("cc") + "_%d" % h, "H0"], ["p_ta"], ["ta"])
             if not last:
-                V(nm("kn"), CH, lambda g, T, base=base: g.vector.tensor_scalar(T.kout[:, base:base + CH], mr(T, 7), col(T, "kc"), None, A.add),
-                  ["m7", "c_kc"], ["kout%d_%d" % (e, c)], ["bm"])
+                V(nm("kn"), CH, lambda g, T, base=base: g.vector.tensor_scalar(T.kout[:, base:base + CH], T.ta[:, 0:CH], col(T, "kc"), None, A.add),
+                  ["p_ta", "c_kc"], ["kout%d_%d" % (e, c)], ["ta"])
                 op("G", nm("sk"), 1.0, ("send", "k", e, c, base), R=["kout%d_%d" % (e, c)], W=["sentk%d_%d" % (e + 1, c)])
             else:
-                V(nm("kn"), CH, lambda g, T, c=c: g.vector.tensor_scalar(T.ykb[:, CH * c:CH * c + CH], mr(T, 7), col(T, "kc"), None, A.add),
-                  ["m7", "c_kc"], ["ykb%d" % c], ["bm"])
+                V(nm("kn"), CH, lambda g, T, c=c: g.vector.tensor_scalar(T.ykb[:, CH * c:CH * c + CH], T.ta[:, 0:CH], col(T, "kc"), None, A.add),
+                  ["p_ta", "c_kc"], ["ykb%d" % c], ["ta"])
                 op("Y", nm("yk"), 0.1, lambda g, T, c=c: g.sync.dma_start(T.yk[:, CH * c:CH * c + CH], T.ykb[:, CH * c:CH * c + CH]),
                    R=["ykb%d" % c], W=["yk%d" % c], lat=2.0)
-            P(nm("wb"), 1, lambda g, T, hh=hh: g.tensor.matmul(mr(T, 1), h16(T, 0), hh(T, 3), True, True), [t("b"), "H0", t("sg")], ["m1"], ["bm"])
-            V(nm("bfd"), CH, lambda g, T, hh=hh: g.vector.tensor_tensor(hh(T, 2), mr(T, 1), hh(T, 1), A.mult), ["m1", t("fd")], [t("bfd")], ["bm"])
+            P(nm("wb"), 1, lambda g, T, hh=hh: g.tensor.matmul(mr(T, 3), h16(T, 0), hh(T, 3), True, True), [t("b"), "H0", t("sg")], ["m3"], ["bm"])
+            V(nm("bfd"), CH, lambda g, T, hh=hh: g.vector.tensor_tensor(hh(T, 2), mr(T, 3), hh(T, 1), A.mult), ["m3", t("fd")], [t("bfd")], ["bm"])
 
             def pw(g, T, hh=hh):
-                g.tensor.matmul(mr(T, 2), h16(T, 0), hh(T, 1), True, False)
-                g.tensor.matmul(mr(T, 2), h16(T, 2), hh(T, 2), False, True)
-                g.tensor.matmul(mr(T, 3), h16(T, 1), hh(T, 1), True, False)
-                return g.tensor.matmul(mr(T, 3), h16(T, 0), hh(T, 2), False, True)
-            P(nm("pw"), 4, pw, [t("fd"), t("bfd"), "H0", "H1", "H2"], ["m2", "m3"], ["bm"])
-            V(nm("wu"), 2 * CH, lambda g, T, gw=gw: g.vector.tensor_tensor(gw(T, 1, 2), mr(T, 2, 2), gw(T, 1, 2), A.add),
-              ["m2", "m3", t("gw1_"), t("gw2_")], [t("gw1_"), t("gw2_")], ["bm"])
+                g.tensor.matmul(mr(T, 1), h16(T, 0), hh(T, 1), True, False)
+                g.tensor.matmul(mr(T, 1), h16(T, 2), hh(T, 2), False, True)
+                g.tensor.matmul(mr(T, 2), h16(T, 1), hh(T, 1), True, False)
+                return g.tensor.matmul(mr(T, 2), h16(T, 0), hh(T, 2), False, True)
+            P(nm("pw"), 4, pw, [t("fd"), t("bfd"), "H0", "H1", "H2"], ["m1", "m2"], ["bm"])
+            V(nm("wu"), 2 * CH, lambda g, T, gw=gw: g.vector.tensor_tensor(gw(T, 2, 2), mr(T, 1, 2), gw(T, 2, 2), A.add),
+              ["m1", "m2", t("gw2_"), t("gw3_")], [t("gw2_"), t("gw3_")], ["bm"])
             if last:
                 o = 2 * CH * c
-                V(nm("w0"), CH, lambda g, T, gw=gw, o=o: g.vector.tensor_copy(T.ywb[:, o:o + 2 * CH:2], gw(T, 2)), [t("gw2_")], ["yw0%d" % c])
-                V(nm("w1"), 2 * CH, lambda g, T, gw=gw, o=o: g.vector.tensor_tensor(T.ywb[:, o + 1:o + 2 * CH:2], gw(T, 2), gw(T, 1), A.add),
-                  [t("gw1_"), t("gw2_")], ["yw1%d" % c])
+                V(nm("w0"), CH, lambda g, T, gw=gw, o=o: g.vector.tensor_copy(T.ywb[:, o:o + 2 * CH:2], gw(T, 3)), [t("gw3_")], ["yw0%d" % c])
+                V(nm("w1"), 2 * CH, lambda g, T, gw=gw, o=o: g.vector.tensor_tensor(T.ywb[:, o + 1:o + 2 * CH:2], gw(T, 3), gw(T, 2), A.add),
+                  [t("gw2_"), t("gw3_")], ["yw1%d" % c])
                 op("Y", nm("yw"), 0.1, lambda g, T, o=o: g.sync.dma_start(T.yw[:, o:o + 2 * CH], T.ywb[:, o:o + 2 * CH]),
                    R=["yw0%d" % c, "yw1%d" % c], W=["yw%d" % c], lat=2.0)
             if c == NC - 1 and not last:
-                V(nm("fa"), 6, lambda g, T: g.vector.tensor_copy(T.accb[:], T.acc[:]), ["acc%d" % j for j in range(6)], ["accb"])
+                V(nm("fa"), NC, lambda g, T: g.vector.tensor_copy(T.accb[:], T.acc[:]), ["acc%d" % j for j in range(NC)], ["accb"])
 
                 def ft(g, T):
-                    for j in range(6):
-                        r = g.tensor.matmul(T.bf[:, 448:449], mat(T, "ONE" if j < 3 else "nONE"), T.accb[:, j:j + 1], j == 0, j == 5)
+                    for j in range(NC):
+                        r = g.tensor.matmul(T.bf[:, 448:449], mat(T, "ONE"), T.accb[:, j:j + 1], j == 0, j == NC - 1)
                     return r
-                P(nm("ft"), 6, ft, ["accb", "ONE", "nONE"], ["f7"], ["bf"])
+                P(nm("ft"), NC, ft, ["accb", "ONE"], ["f7"], ["bf"])
                 V(nm("fi"), 1, lambda g, T: g.vector.tensor_copy(T.fi[:, 0:1], T.bf[:, 448:449]), ["f7"], ["fi"], ["bf"])
                 V(nm("fj"), 1, lambda g, T: g.vector.tensor_scalar(T.fj[:, 0:1], T.fi[:, 0:1], 31, None, A.bitwise_and), ["fi"], ["fj"])
                 V(nm("tA"), 1, lambda g, T: g.vector.tensor_scalar(col(T, "thA"), T.fj[:, 0:1], 16.0, col(T, "thm"), A.mult, A.add),
@@ -560,7 +560,7 @@ PLAN = {}
 def plan():
     if "ops" not in PLAN:
         ops = build()
-        order, end = schedule(ops, modulo(ops, PER)[0], PER)
+        order, end = schedule(ops)
         glob = sorted((o["start"], o["k"]) for o in ops)
         PLAN["ops"] = ops
         PLAN["glob"] = [k for _, k in glob]

from concourse.bass import DstId, RemoteDMATransfer
from concourse.mybir import dt, AluOpType, AxisListType, ActivationFunctionType
import math

A = AluOpType
AF = ActivationFunctionType
LE = 6
NC = 3
CH = 64
FULL = 16 * CH
GAM = 1.5
CY = 0.00083
PC = 0.00042
AHEAD = 0.0
PER = 12.0
BIAS = {'k32': 0.6, 'T1': -2.1, 'cs0': -2.3, 'pw': 12.0, 'cl0': -14.0, 'dg3': -3.1, 'sk': 13.1, 'po': 3.3, 'ko': -1.0, 'sz': -1.1,
        'tA': 3.6, 'sgea1': 2.8, 'm1': 3.2, 'fa': 5.6, 'sgeb0': 0.6, 'w1': -11.1, 'mkeb': 5.0, 'r5': 1.6, 'Eeb': -0.6, 'ab3': 2.7,
        'bd': 1.3, 'cl1': 0.5, 'nz': -1.6, 'sg': 1.8, 'sgea0': 0.5, 'ph': 3.2, 'R2': 13.8, 'dp': 5.8, 'ab0': -0.4, 'w0': -0.5,
        'fc': -6.0, 'bb': 11.2, 'mkea': 0.9, 'fj': 2.2, 'R3': 1.7, 'wu': 1.2, 'bfd': 0.6, 'vs': 1.1, 'ab2': -0.6, 'cs1': -2.4,
        'thr': 0.4, 't2': 0.7, 't4': 0.4, 't3': 0.9, 'hs': -0.2, 'za': -0.2, 'r3': 0.1, 'wb': 0.1, 'fd': -0.1, 'nu': -0.1}
XP = 4
SCB = True
WAKE = 0.17

SCRATCH = {
    "gxb": ("sbuf", [128, 2048], "bfloat16"), "syb": ("sbuf", [128, 2048], "bfloat16"),
    "rkb": ("sbuf", [128, 192], "int32"), "rtb": ("sbuf", [128, 384], "int32"), "wrb": ("sbuf", [128, 384], "int32"),
    "wtb": ("sbuf", [128, 1], "bfloat16"), "thb": ("sbuf", [128, 1], "int32"),
    "kin": ("sbuf", [128, LE * 192], "float16"), "zin": ("sbuf", [128, LE * 192], "bfloat16"),
    "kout": ("sbuf", [128, LE * 192], "float16"), "zout": ("sbuf", [128, LE * 192], "bfloat16"),
    "ykb": ("sbuf", [128, 192], "float32"), "ywb": ("sbuf", [128, 384], "float32"),
    "pid": ("sbuf", [128, 1], "int32"), "pki": ("sbuf", [128, 1], "int32"), "pgi": ("sbuf", [128, 1], "int32"),
    "mq": ("sbuf", [128, 128], "float32"), "mg": ("sbuf", [128, 128], "float32"), "mi": ("sbuf", [128, 128], "float32"),
    "tq0": ("sbuf", [128, 128], "float32"),
    "cols": ("sbuf", [128, 16], "float32"), "rmn": ("sbuf", [128, 16], "float32"), "rm1": ("sbuf", [128, 16], "float32"),
    "w37": ("sbuf", [128, 1], "int32"), "w37l": ("sbuf", [128, 1], "int32"),
    "mats": ("sbuf", [128, 24 * 128], "bfloat16"), "m16": ("sbuf", [128, 4 * 128], "float16"),
    "on16": ("sbuf", [128, CH], "float16"),
    "bc": ("sbuf", [128, 2048], "bfloat16"), "bv": ("sbuf", [128, 2048], "float16"),
    "bk": ("sbuf", [128, 2048], "bfloat16"), "tp": ("sbuf", [128, 2048], "bfloat16"),
    "rst": ("sbuf", [128, 512], "bfloat16"),
    "acc": ("sbuf", [128, NC], "float32"), "accb": ("sbuf", [128, NC], "bfloat16"),
    "fi": ("sbuf", [128, 1], "int32"), "fj": ("sbuf", [128, 1], "int32"),
    "ea0": ("psum", [128, 512], "float32"), "eb0": ("psum", [128, 512], "float32"),
    "ea1": ("psum", [128, 512], "float32"), "eb1": ("psum", [128, 512], "float32"),
    "ta": ("psum", [128, 512], "float32"), "tb": ("psum", [128, 512], "float32"),
    "bf": ("psum", [128, 512], "float32"), "bm": ("psum", [128, 512], "float32"),
}
for _c in range(NC):
    for _n, _w, _d in (("gw", 4 * CH, "float16"), ("ko", CH, "uint16"), ("so", CH, "uint16"), ("xg", FULL, "bfloat16"),
                       ("dg", FULL, "bfloat16"), ("ab", FULL, "bfloat16"), ("cc", FULL, "float16"),
                       ("ii", 4 * CH, "int32"), ("tt", 9 * CH, "int32"), ("hh", 4 * CH, "float16"), ("bd", CH, "float16"), ("thr", CH, "float32"),
                       ("sm", 12 * CH, "bfloat16")):
        SCRATCH["%s%d" % (_n, _c)] = ("sbuf", [128, _w], _d)
    for _n in ("ha", "hb", "ra", "rb", "eb"):
        SCRATCH["%s%d" % ("e_" if _n == "eb" else _n, _c)] = ("sbuf", [128, 512], "bfloat16")

LOADS = ["rk", "z0", "wt", "gx", "rt", "wr", "th", "sy"]
SEMAPHORES = ["sv", "ss", "sp", "sg", "loc", "fin"] + ["ld_" + x for x in LOADS] + \
    ["az%d_%d" % (e, c) for e in range(1, LE) for c in range(NC)] + ["ak%d_%d" % (e, c) for e in range(1, LE) for c in range(NC)]

MAT = ["BLK", "I", "nI", "I128", "I512", "n128I", "GE", "L2", "U", "L", "LP", "UM", "nU", "U2", "DK", "ONE", "nONE", "TQ", "W", "WH", "WL",
       "I4", "IT", "x1"]
COL = ["p", "k", "g", "b2", "b3", "pos", "kc", "thm", "thA", "wh", "wl"]
SEM = {"V": "sv", "S": "ss", "P": "sp", "G": "sg"}


def build():
    ops = []
    lastw, readers = {}, {}

    def op(eng, name, cost, fn, R=(), W=(), banks=(), lat=0.0, sem=None):
        k = len(ops)
        deps, soft = set(), set()
        for r in R:
            if r in lastw:
                deps.add(lastw[r])
        for w in W:
            if w in lastw:
                deps.add(lastw[w])
            for x in readers.get(w, ()):
                soft.add(x)
        o = {"k": k, "eng": eng, "name": name, "cost": cost, "fn": fn, "deps": deps, "soft": soft - deps, "banks": list(banks),
             "lat": lat, "sem": sem}
        ops.append(o)
        for r in R:
            readers.setdefault(r, []).append(k)
        for w in W:
            lastw[w] = k
            readers[w] = []
        return k

    vc = lambda n: max(64, n) * CY
    sc = lambda n: max(64, n) * CY
    ga = lambda n: 0.05 + GAM * n * CY
    mm = lambda n: n * 64 * PC
    col = lambda T, n: T.cols[:, COL.index(n):COL.index(n) + 1]
    mat = lambda T, n: T.mats[:, 128 * MAT.index(n):128 * MAT.index(n) + 128]
    h16 = lambda T, n: T.m16[:, 128 * n:128 * n + 128]

    for x, t in (("rk", 2.2), ("z0", 2.2), ("wt", 2.2), ("gx", 5.0), ("rt", 3.5), ("wr", 3.8), ("th", 3.0), ("sy", 7.0)):
        op("N", "ld_" + x, t, None, W=["zin0_%d" % c for c in range(NC)] if x == "z0" else ["in_" + x], sem=("ld_" + x, 16))

    op("G", "pid", 0.14, lambda g, T: g.iota(T.pid[:, 0:1], [[1, 1]], 0, 1), W=["pid"])
    op("G", "mi", 0.35, lambda g, T: g.iota(T.mi[:], [[1, 128]], 0, 0, allow_small_or_imprecise_dtypes=True), W=["mi"])
    op("G", "mg", 0.35, lambda g, T: g.iota(T.mg[:], [[1, 8], [0, 16]], 0, 0, allow_small_or_imprecise_dtypes=True), W=["mg"])
    op("G", "mq", 0.35, lambda g, T: g.iota(T.mq[:], [[0, 8], [1, 16]], 0, 0, allow_small_or_imprecise_dtypes=True), W=["mq"])
    V = lambda name, n, fn, R=(), W=(), banks=(), cost=None: op("V", name, vc(n) if cost is None else cost, fn, R, W, banks)
    S = lambda name, n, fn, R=(), W=(), banks=(), cost=None: op("S", name, sc(n) if cost is None else cost, fn, R, W, banks)
    P = lambda name, n, fn, R=(), W=(), banks=(): op("P", name, mm(n), fn, R, W, banks)
    V("pki", 1, lambda g, T: g.vector.tensor_scalar(T.pki[:, 0:1], T.pid[:, 0:1], 15, None, A.bitwise_and), ["pid"], ["pki"])
    V("pgi", 1, lambda g, T: g.vector.tensor_scalar(T.pgi[:, 0:1], T.pid[:, 0:1], 4, None, A.arith_shift_right), ["pid"], ["pgi"])
    V("cp", 1, lambda g, T: g.vector.tensor_copy(col(T, "p"), T.pid[:, 0:1]), ["pid"], ["c_p"])
    V("cg", 1, lambda g, T: g.vector.tensor_copy(col(T, "g"), T.pgi[:, 0:1]), ["pgi"], ["c_g"])
    V("ck", 1, lambda g, T: g.vector.tensor_copy(col(T, "k"), T.pki[:, 0:1]), ["pki"], ["c_k"])
    V("BLK", 128, lambda g, T: g.vector.tensor_scalar(mat(T, "BLK"), T.mg[:], col(T, "g"), None, A.is_equal), ["mg", "c_g"], ["BLK"])
    V("W", 64, lambda g, T: g.vector.tensor_scalar(mat(T, "W"), mat(T, "BLK"), T.wtb[:, 0:1], None, A.mult), ["BLK", "in_wt"], ["W"])

    def diag(name, s):
        V(name, 128, lambda g, T: g.vector.tensor_scalar(mat(T, name), T.mi[:], col(T, "p"), float(s), A.is_equal, A.mult),
          ["mi", "c_p"], [name])
    diag("I", 1.0)
    V("on16", CH, lambda g, T: g.vector.tensor_scalar(T.on16[:], T.mi[:, 0:CH], 0.0, 1.0, A.mult, A.add), ["mi"], ["on16"])
    for j, s in enumerate((1.0, -1.0, -2.0, 32.0)):
        V("H%d" % j, 128, lambda g, T, j=j, s=s: g.vector.tensor_scalar(h16(T, j), T.mi[:], col(T, "p"), s, A.is_equal, A.mult),
          ["mi", "c_p"], ["H%d" % j])
    V("w37", 1, lambda g, T: g.vector.tensor_scalar(T.w37[:, 0:1], T.wtb[:, 0:1], 37.0, None, A.mult), ["in_wt"], ["w37"])
    V("w37l", 1, lambda g, T: g.vector.tensor_scalar(T.w37l[:, 0:1], T.w37[:, 0:1], 15, None, A.bitwise_and), ["w37"], ["w37l"])
    V("wl", 1, lambda g, T: g.vector.tensor_copy(col(T, "wl"), T.w37l[:, 0:1]), ["w37l"], ["c_wl"])
    V("wh", 1, lambda g, T: g.vector.tensor_tensor(col(T, "wh"), T.w37[:, 0:1], T.w37l[:, 0:1], A.subtract), ["w37", "w37l"], ["c_wh"])
    V("WH", 64, lambda g, T: g.vector.tensor_scalar(mat(T, "WH"), mat(T, "BLK"), col(T, "wh"), None, A.mult), ["BLK", "c_wh"], ["WH"])
    V("WL", 64, lambda g, T: g.vector.tensor_scalar(mat(T, "WL"), mat(T, "BLK"), col(T, "wl"), None, A.mult), ["BLK", "c_wl"], ["WL"])
    diag("nI", -1.0)
    V("rmn", 16, lambda g, T: g.vector.tensor_scalar(T.rmn[:], T.mq[:, 0:16], col(T, "k"), -512.0, A.is_equal, A.mult), ["mq", "c_k"], ["rmn"])
    V("rm1", 16, lambda g, T: g.vector.tensor_scalar(T.rm1[:], T.mq[:, 0:16], col(T, "k"), None, A.is_equal), ["mq", "c_k"], ["rm1"])
    for k in range(16):
        S("bc%d" % k, 128, lambda g, T, k=k: g.scalar.activation(T.bc[:, 128 * k:128 * k + 128], mat(T, "BLK"), AF.Copy,
                                                                 scale=T.rmn[:, k:k + 1]), ["BLK", "rmn"], ["bc%d" % k])
    diag("IT", -1.0 / 512)
    for q in range(4):
        def trs(g, T, q=q):
            o = T.ta if q % 2 == 0 else T.tb
            for j in range(4):
                k = 4 * q + j
                r = g.tensor.matmul(o[:, 128 * j:128 * j + 128], T.bc[:, 128 * k:128 * k + 128], mat(T, "IT"), True, True)
            return r
        b = "ta" if q % 2 == 0 else "tb"
        P("trs%d" % q, 8, trs, ["IT"] + ["bc%d" % k for k in range(4 * q, 4 * q + 4)], ["p_" + b], [b])
        S("bk%d" % q, 512, lambda g, T, q=q: g.scalar.activation(T.bk[:, 512 * q:512 * q + 512], (T.ta if q % 2 == 0 else T.tb)[:], AF.Copy),
          ["p_" + b], ["bk%d" % q], [b])
    diag("I128", 128.0)
    diag("I512", 512.0)
    diag("n128I", -128.0)
    V("GE0", 128, lambda g, T: g.vector.tensor_scalar(mat(T, "x1"), T.mi[:], col(T, "p"), None, A.is_le), ["mi", "c_p"], ["x1"])
    tt = lambda name, a, b, o: V(name, 256, lambda g, T: g.vector.tensor_tensor(mat(T, name), mat(T, a), mat(T, b), o), [a, b], [name])
    tt("GE", "x1", "BLK", A.mult)
    tt("U", "GE", "I", A.subtract)
    tt("L", "BLK", "GE", A.subtract)
    for n, x, s in (("L2", "L", 2.0), ("nU", "U", -2.0), ("U2", "U", 2.0)):
        V(n, 64, lambda g, T, n=n, x=x, s=s: g.vector.tensor_scalar(mat(T, n), mat(T, x), s, None, A.mult), [x], [n])
    tt("LP", "L2", "I128", A.add)
    tt("UM", "U2", "I128", A.subtract)
    for n, a, b in (("b3", 2.0, 1.0), ("pos", -2.0, 31.0), ("kc", 2048.0, -30720.0)):
        V("c_" + n, 1, lambda g, T, n=n, a=a, b=b: g.vector.tensor_scalar(col(T, n), col(T, "k"), a, b, A.mult, A.add), ["c_k"], ["c_" + n])
    V("DK", 64, lambda g, T: g.vector.tensor_scalar(mat(T, "DK"), mat(T, "I"), col(T, "pos"), None, A.mult), ["I", "c_pos"], ["DK"])
    V("thm", 1, lambda g, T: g.vector.tensor_scalar(col(T, "thm"), T.thb[:, 0:1], -0.5, None, A.add), ["in_th"], ["c_thm"])
    V("ONE", 64, lambda g, T: g.vector.memset(mat(T, "ONE"), 1.0), [], ["ONE"])
    V("nONE", 64, lambda g, T: g.vector.memset(mat(T, "nONE"), -1.0), [], ["nONE"])
    V("rst0", 256, lambda g, T: g.vector.memset(T.rst[:], 1.0), [], ["rst"])
    V("rst1", 64, lambda g, T: g.vector.memset(T.rst[:, 0::8], 0.0), [], ["rst"])
    V("tq0", 128, lambda g, T: g.vector.tensor_scalar(T.tq0[:], T.mq[:], -16.0, -8.0, A.mult, A.add), ["mq"], ["tq0"])
    V("TQ", 256, lambda g, T: g.vector.tensor_tensor(mat(T, "TQ"), T.tq0[:], mat(T, "BLK"), A.mult), ["tq0", "BLK"], ["TQ"])
    diag("I4", -4.0)
    for k in range(16):
        V("bv%d" % k, 64, lambda g, T, k=k: g.vector.tensor_scalar(T.bv[:, 128 * k:128 * k + 128], mat(T, "BLK"), T.rm1[:, k:k + 1], None, A.mult),
          ["BLK", "rm1"], ["bv%d" % k])
    for q in range(4):
        def tps(g, T, q=q):
            o = T.ta if q % 2 == 0 else T.tb
            for j in range(4):
                k = 4 * q + j
                g.tensor.matmul(o[:, 128 * j:128 * j + 128], mat(T, "I4"), T.bc[:, 128 * k:128 * k + 128], True, False)
                r = g.tensor.matmul(o[:, 128 * j:128 * j + 128], mat(T, "I"), mat(T, "TQ"), False, True)
            return r
        b = "ta" if q % 2 == 0 else "tb"
        P("tps%d" % q, 16, tps, ["I", "I4", "TQ"] + ["bc%d" % k for k in range(4 * q, 4 * q + 4)], ["p_" + b, "p_" + b + "0", "p_" + b + "1"], [b])
        S("tp%d" % q, 512, lambda g, T, q=q: g.scalar.activation(T.tp[:, 512 * q:512 * q + 512], (T.ta if q % 2 == 0 else T.tb)[:], AF.Copy),
          ["p_" + b, "p_" + b + "0", "p_" + b + "1"], ["tp%d" % q], [b])

    for c in range(NC):
        sl = slice(CH * c, CH * c + CH)
        V("k0_%d" % c, CH, lambda g, T, sl=sl: g.vector.tensor_copy(T.kin[:, sl], T.rkb[:, sl]), ["in_rk"], ["kin0_%d" % c])
        ev, od = slice(2 * CH * c, 2 * CH * c + 2 * CH, 2), slice(2 * CH * c + 1, 2 * CH * c + 2 * CH, 2)
        for src, base, cut in (("rt", 0, ev), ("rt", 1, od), ("wr", 3, ev)):
            V("%s%d_%d" % (src, base, c), CH, lambda g, T, c=c, src=src, base=base, cut=cut:
              g.vector.tensor_copy(T["gw%d" % c][:, CH * base:CH * base + CH], T[src + "b"][:, cut]), ["in_" + src], ["gw%d_%d" % (base, c)])
        V("wrd%d" % c, 2 * CH, lambda g, T, c=c, ev=ev, od=od: g.vector.tensor_tensor(
            T["gw%d" % c][:, CH * 2:CH * 3], T.wrb[:, od], T.wrb[:, ev], A.subtract), ["in_wr"], ["gw2_%d" % c])

    fr = lambda T, j, n=1: T.bf[:, 64 * j:64 * j + 64 * n]
    mr = lambda T, j, n=1: T.bm[:, 64 * j:64 * j + 64 * n]
    for e in range(LE):
        for c in range(NC):
            n = NC * e + c
            es = str(n % 2)
            base = 192 * e + CH * c
            kin = lambda T, b=base: T.kin[:, b:b + CH]
            zin = lambda T, b=base: T.zin[:, b:b + CH]
            K_, Z_ = "kin%d_%d" % (e, c), "zin%d_%d" % (e, c)
            t = lambda x, c=c: "%s%d" % (x, c)
            sm = lambda T, j, c=c: T["sm%d" % c][:, CH * j:CH * j + CH]
            ii = lambda T, j, c=c: T["ii%d" % c][:, CH * j:CH * j + CH]
            tb = lambda T, j, m=1, c=c: T["tt%d" % c][:, CH * j:CH * j + CH * m]
            hh = lambda T, j, c=c: T["hh%d" % c][:, CH * j:CH * j + CH]
            gw = lambda T, j, m=1, c=c: T["gw%d" % c][:, CH * j:CH * j + CH * m]
            nm = lambda x, e=e, c=c: "%s.%d.%d" % (x, e, c)
            if e > 0:
                op("N", nm("az"), 2.5, None, R=["sentz%d_%d" % (e, c)], W=[Z_], sem=("az%d_%d" % (e, c), 0))
                op("N", nm("ak"), 2.5, None, R=["sentk%d_%d" % (e, c)], W=[K_], sem=("ak%d_%d" % (e, c), 0))
            V(nm("ko"), CH, lambda g, T, t=t, kin=kin: g.vector.tensor_copy(T[t("ko")][:], kin(T)), [K_], [t("ko")])
            for q in range(XP):
                a, b = FULL // XP * q, FULL // XP * (q + 1)
                S(nm("xg%d" % q), 0, lambda g, T, t=t, q=q, a=a, b=b: g.scalar.activation(
                    T[t("xg")][:, a:b], T.gxb[:].indirect(T[t("ko")][:, a // 16:b // 16]), AF.Copy),
                  [t("ko"), "in_gx"], [t("xg") + "_%d" % q], cost=0.065 + GAM * FULL // XP * CY)
            XG = [t("xg") + "_%d" % q for q in range(XP)]
            P(nm("U"), 1, lambda g, T, zin=zin: g.tensor.matmul(fr(T, 0), mat(T, "W"), zin(T), True, True), [Z_, "W"], ["f0"], ["bf"])
            V(nm("r1"), CH, lambda g, T, ii=ii: g.vector.tensor_copy(ii(T, 0), fr(T, 0)), ["f0"], [t("ii0")], ["bf"])
            V(nm("r2"), CH, lambda g, T, ii=ii: g.vector.tensor_scalar(ii(T, 1), ii(T, 0), 63, None, A.bitwise_and), [t("ii0")], [t("ii1")])
            V(nm("r3"), 2 * CH, lambda g, T, ii=ii: g.vector.tensor_tensor(ii(T, 2), ii(T, 1), ii(T, 1), A.mult), [t("ii1")], [t("ii2")])
            V(nm("r4"), CH, lambda g, T, ii=ii: g.vector.tensor_scalar(ii(T, 3), ii(T, 2), 5, 1, A.arith_shift_right, A.bitwise_and),
              [t("ii2")], [t("ii3")])
            V(nm("r5"), CH, lambda g, T, ii=ii, hh=hh: g.vector.tensor_copy(hh(T, 3), ii(T, 3)), [t("ii3")], [t("b")])

            def k32(g, T, kin=kin):
                for j in (3, 4):
                    g.tensor.matmul(fr(T, j), h16(T, 3), T.on16[:], True, False)
                    r = g.tensor.matmul(fr(T, j), h16(T, 0), kin(T), False, True)
                return r
            P(nm("k32"), 4, k32, [K_, "H0", "H3", "on16"], ["f3"], ["bf"])

            def u37(g, T, zin=zin):
                g.tensor.matmul(fr(T, 5), mat(T, "WH"), zin(T), True, False)
                return g.tensor.matmul(fr(T, 5), mat(T, "WL"), zin(T), False, True)
            P(nm("u37"), 2, u37, [Z_, "WH", "WL"], ["f5"], ["bf"])
            V(nm("t1"), 2 * CH, lambda g, T, tb=tb, gw=gw: g.vector.tensor_tensor(tb(T, 0, 2), fr(T, 3, 2), gw(T, 0, 2), A.mult),
              ["f3", t("gw0_"), t("gw1_")], [t("t0")], ["bf"])
            V(nm("t2"), 2 * CH, lambda g, T, tb=tb: g.vector.tensor_scalar(tb(T, 2, 2), tb(T, 0, 2), 5, None, A.arith_shift_right), [t("t0")], [t("t1")])
            V(nm("dp"), 2 * CH, lambda g, T, tb=tb: g.vector.tensor_tensor(tb(T, 4), tb(T, 3), tb(T, 2), A.subtract), [t("t1")], [t("dp")])
            V(nm("pu"), CH, lambda g, T, tb=tb: g.vector.tensor_tensor(tb(T, 5), fr(T, 5), tb(T, 2), A.add), [t("t1"), "f5"], [t("pu")], ["bf"])
            V(nm("bp"), 2 * CH, lambda g, T, tb=tb, ii=ii: g.vector.tensor_tensor(tb(T, 6), tb(T, 4), ii(T, 3), A.mult), [t("dp"), t("ii3")], [t("bp")])
            V(nm("t3"), 2 * CH, lambda g, T, tb=tb: g.vector.tensor_tensor(tb(T, 7), tb(T, 6), tb(T, 5), A.add), [t("bp"), t("pu")], [t("t2")])
            V(nm("t4"), CH, lambda g, T, tb=tb: g.vector.tensor_scalar(tb(T, 8), tb(T, 7), 2047, None, A.bitwise_and), [t("t2")], [t("t3")])
            V(nm("so"), CH, lambda g, T, t=t, tb=tb: g.vector.tensor_copy(T[t("so")][:], tb(T, 8)), [t("t3")], [t("so")])
            P(nm("fb"), 1, lambda g, T, hh=hh: g.tensor.matmul(fr(T, 1), h16(T, 0), hh(T, 3), True, True), [t("b"), "H0"], ["f1"], ["bf"])
            V(nm("bd"), CH, lambda g, T, t=t, gw=gw: g.vector.tensor_tensor(T[t("bd")][:], fr(T, 1), gw(T, 2), A.mult),
              ["f1", t("gw2_")], [t("bd")], ["bf"])

            def od(g, T, t=t, gw=gw, kin=kin):
                g.tensor.matmul(mr(T, 4), h16(T, 0), gw(T, 3), True, False)
                g.tensor.matmul(mr(T, 4), h16(T, 1), kin(T), False, False)
                return g.tensor.matmul(mr(T, 4), h16(T, 0), T[t("bd")][:], False, True)
            for q in range(XP):
                a, b = FULL // XP * q, FULL // XP * (q + 1)
                V(nm("dg%d" % q), 0, lambda g, T, t=t, q=q, a=a, b=b: g.vector.tensor_tensor(
                    T[t("dg")][:, a:b], T.syb[:].indirect(T[t("so")][:, a // 16:b // 16]), T[t("xg")][:, a:b], A.subtract),
                  [t("so"), t("xg") + "_%d" % q, "in_sy"], [t("dg") + "_%d" % q], cost=ga(FULL // XP))
                S(nm("ab%d" % q), FULL // XP, lambda g, T, t=t, a=a, b=b: g.scalar.activation(T[t("ab")][:, a:b], T[t("dg")][:, a:b], AF.Abs),
                  [t("dg") + "_%d" % q], [t("ab") + "_%d" % q])
            for bank, k0, hb in (("ea0", 0, "ha"), ("eb0", 8, "hb")):
                def ez(g, T, bank=bank, k0=k0, t=t, zin=zin):
                    for kk in range(8):
                        o = T[bank][:, CH * kk:CH * kk + CH]
                        g.tensor.matmul(o, mat(T, "I"), T[t("xg")][:, k0 + kk::16], True, False)
                        r = g.tensor.matmul(o, mat(T, "nI"), zin(T), False, True)
                    return r
                P(nm("E" + bank[:2]), 16, ez, XG + [Z_, "I", "nI"], ["p_" + bank], [bank])
                for a in range(2):
                    def sgn(g, T, bank=bank, hb=hb, a=a, t=t, k0=k0):
                        for kk in (4 * a, 4 * a + 2):
                            m = 16 * ((15 - (k0 + kk)) // 2)
                            r = g.scalar.activation(T[t(hb)][:, CH * kk:CH * kk + 2 * CH], T[bank][:, CH * kk:CH * kk + 2 * CH], AF.Sign, bias=0.5 - m)
                        return r
                    S(nm("sg%s%d" % (bank[:2], a)), 4 * CH, sgn, ["p_" + bank], [t(hb) + "_%d" % a], [bank])
            EB = [("ea1", 0), ("eb1", 8)]
            for bank, k0 in EB:
                def ex(g, T, bank=bank, k0=k0, t=t):
                    for kk in range(8):
                        r = g.tensor.matmul(T[bank][:, kk::8], mat(T, "I"), T[t("xg")][:, k0 + kk::16], kk == 0, False)
                    return r
                P(nm("X" + bank[:2]), 8, ex, XG + ["I"], ["p_" + bank], [bank])

            def dsum(g, T, t=t):
                for k in range(16):
                    r = g.tensor.matmul(fr(T, 6), T.bk[:, 128 * k:128 * k + 128], T[t("ab")][:, k::16], k == 0, k == 15)
                return r
            P(nm("ds"), 16, dsum, [t("ab") + "_%d" % q for q in range(XP)] + ["bk%d" % q for q in range(4)], ["f6"], ["bf"])

            def hsum(g, T, t=t):
                for k in range(16):
                    r = g.tensor.matmul(mr(T, 0), T.bk[:, 128 * k:128 * k + 128], T[t("ha" if k < 8 else "hb")][:, CH * (k % 8):CH * (k % 8) + CH], k == 0, k == 15)
                return r
            P(nm("hs"), 16, hsum, [t(x) + "_%d" % a for x in ("ha", "hb") for a in range(2)] + ["bk%d" % q for q in range(4)], ["m0"], ["bm"])
            th = "c_thm" if e == 0 else "c_thA"
            tcol = "thm" if e == 0 else "thA"
            V(nm("thr"), CH, lambda g, T, t=t, tcol=tcol: g.vector.tensor_scalar(T[t("thr")][:], mr(T, 0), 1.0, col(T, tcol), A.is_gt, A.mult),
              ["m0", th], [t("thr")], ["bm"])
            V(nm("ph"), CH, lambda g, T, t=t, sm=sm: g.vector.tensor_tensor(sm(T, 2), fr(T, 6), T[t("thr")][:], A.is_lt),
              ["f6", t("thr")], [t("ph")], ["bf"])
            V(nm("pl"), CH, lambda g, T, sm=sm, tcol=tcol: g.vector.tensor_scalar(sm(T, 1), fr(T, 6), col(T, tcol), None, A.is_lt),
              ["f6", th], [t("pl")], ["bf"])

            def vs(g, T, sm=sm):
                for o in (fr(T, 2), mr(T, 3)):
                    g.tensor.matmul(o, mat(T, "GE"), sm(T, 2), True, False)
                    r = g.tensor.matmul(o, mat(T, "I512"), sm(T, 1), False, True)
                return r
            P(nm("vs"), 4, vs, [t("ph"), t("pl"), "GE", "I512"], ["f2", "m3"], ["bf", "bm"])
            V(nm("nu"), CH, lambda g, T, sm=sm: g.vector.tensor_scalar(sm(T, 7), fr(T, 2), 512.5, None, A.is_lt), ["f2"], [t("nu")], ["bf"])
            V(nm("fl"), CH, lambda g, T, sm=sm: g.vector.tensor_scalar(sm(T, 11), fr(T, 2), 512.0, None, A.is_equal), ["f2"], [t("fl")], ["bf"])
            S(nm("sg"), CH, lambda g, T, sm=sm: g.scalar.activation(sm(T, 3), mr(T, 3), AF.Sign, bias=-512.0), ["m3"], [t("sg")], ["bm"])
            S(nm("fc"), CH, lambda g, T, sm=sm, c=c: g.scalar.activation(sm(T, 0), sm(T, 11), AF.Copy, accum_out=T.acc[:, c:c + 1]),
              [t("fl")], [t("fcs"), "acc%d" % c])

            def bb(g, T, sm=sm):
                g.tensor.matmul(mr(T, 1), mat(T, "LP"), sm(T, 1), True, True)
                return g.tensor.matmul(mr(T, 2), mat(T, "UM"), sm(T, 1), True, True)
            P(nm("bb"), 2, bb, [t("pl"), "LP", "UM"], ["m1", "m2"], ["bm"])
            S(nm("R2"), CH, lambda g, T, sm=sm: g.scalar.activation(sm(T, 4), mr(T, 1), AF.Relu, bias=-127.0), ["m1"], [t("R2")], ["bm"])
            S(nm("R3"), CH, lambda g, T, sm=sm: g.scalar.activation(sm(T, 5), mr(T, 2), AF.Relu, bias=col(T, "b3")), ["m2", "c_b3"], [t("R3")], ["bm"])

            def po(g, T, sm=sm):
                g.tensor.matmul(mr(T, 6), mat(T, "I128"), sm(T, 1), True, False)
                g.tensor.matmul(mr(T, 6), mat(T, "I"), sm(T, 4), False, False)
                g.tensor.matmul(mr(T, 6), mat(T, "I"), sm(T, 5), False, False)
                g.tensor.matmul(mr(T, 6), mat(T, "n128I"), sm(T, 3), False, True)
                g.tensor.matmul(mr(T, 7), mat(T, "DK"), mat(T, "ONE")[:, 0:CH], True, False)
                g.tensor.matmul(mr(T, 7), mat(T, "nU"), sm(T, 1), False, False)
                return g.tensor.matmul(mr(T, 7), mat(T, "U2"), sm(T, 3), False, True)
            P(nm("po"), 7, po, [t("sg"), t("pl"), t("R2"), t("R3"), "U2", "nU", "I", "I128", "n128I", "DK", "ONE"], ["m6", "m7"], ["bm"])
            S(nm("ry"), CH, lambda g, T, sm=sm: g.scalar.activation(sm(T, 10), mr(T, 6), AF.Relu, bias=-128.0), ["m6"], [t("ry")], ["bm"])
            V(nm("pp"), CH, lambda g, T, sm=sm: g.vector.tensor_tensor(sm(T, 6), mr(T, 7), sm(T, 10), A.max), ["m7", t("ry")], [t("pp")], ["bm"])
            P(nm("od"), 3, od, [t("bd"), t("gw3_"), K_, "H0", "H1", t("xg") + "_0"], ["m4"], ["bm"])
            P(nm("kp"), 1, lambda g, T, kin=kin: g.tensor.matmul(mr(T, 5), h16(T, 0), kin(T), True, True), [K_, "H0", t("xg") + "_0"], ["m5"], ["bm"])
            V(nm("fd"), CH, lambda g, T, hh=hh, sm=sm: g.vector.tensor_tensor(hh(T, 1), mr(T, 4), sm(T, 11), A.mult), ["m4", t("fl")], [t("fd")], ["bm"])
            V(nm("v"), CH, lambda g, T, t=t, hh=hh: g.vector.tensor_tensor(T[t("vv")][:], mr(T, 5), hh(T, 1), A.add), ["m5", t("fd")], [t("v")], ["bm"])
            for bank, k0 in EB:
                def mk(g, T, bank=bank, k0=k0, sm=sm):
                    for kk in range(8):
                        k = k0 + kk
                        r = g.tensor.matmul(T[bank][:, kk::8], T.bc[:, 128 * k:128 * k + 128], sm(T, 7), False, kk == 7)
                    return r
                P(nm("mk" + bank[:2]), 8, mk, [t("nu")] + ["bc%d" % k for k in range(k0, k0 + 8)], ["p_" + bank], [bank])
            bA, bB = EB[0][0], EB[1][0]
            for a, b in ((0, 256), (256, 512)):
                V(nm("sca%d" % (a > 0)), 256, lambda g, T, t=t, bA=bA, a=a, b=b: g.vector.tensor_tensor_scan(
                    T[t("ra")][:, a:b], T.rst[:, a:b], T[bA][:, a:b], 0.0, A.mult, A.max), ["p_" + bA, "rst"], [t("ra") + "_%d" % (a > 0)], [bA])
            if SCB:
                S(nm("eb"), 512, lambda g, T, t=t, bB=bB: g.scalar.activation(T[t("e_")][:], T[bB][:], AF.Copy), ["p_" + bB], [t("e_")], [bB])
                V(nm("scb"), 256, lambda g, T, t=t: g.vector.tensor_tensor_scan(T[t("rb")][:], T.rst[:], T[t("e_")][:], 0.0, A.mult, A.max),
                  [t("e_"), "rst"], [t("rb")])
            else:
                V(nm("scb"), 512, lambda g, T, t=t, bB=bB: g.vector.tensor_tensor_scan(T[t("rb")][:], T.rst[:], T[bB][:], 0.0, A.mult, A.max),
                  ["p_" + bB, "rst"], [t("rb")], [bB])
            P(nm("nz"), 1, lambda g, T, zin=zin: g.tensor.matmul(mr(T, 0), mat(T, "nI"), zin(T), True, True), [Z_, "nI"], ["m0"], ["bm"])
            V(nm("m1"), 2 * CH, lambda g, T, t=t, sm=sm: g.vector.tensor_tensor(sm(T, 8), T[t("ra")][:, 7::8], T[t("rb")][:, 7::8], A.max),
              [t("ra") + "_0", t("ra") + "_1", t("rb")], [t("mx")])
            V(nm("m2"), CH, lambda g, T, sm=sm: g.vector.tensor_tensor(sm(T, 9), mr(T, 0), sm(T, 8), A.add), [t("mx"), "m0"], [t("my")], ["bm"])
            last = e == LE - 1
            S(nm("za"), CH, lambda g, T, sm=sm, base=base: g.scalar.activation(T.zout[:, base:base + CH], sm(T, 9), AF.Abs),
              [t("my")], ["zout%d_%d" % (e, c)])
            if not last:
                op("G", nm("sz"), 1.0, ("send", "z", e, c, base), R=["zout%d_%d" % (e, c)], W=["sentz%d_%d" % (e + 1, c)])
            else:
                op("Y", nm("yz"), 0.1, lambda g, T, base=base, c=c: g.sync.dma_start(T.yz[:, CH * c:CH * c + CH], T.zout[:, base:base + CH]),
                   R=["zout%d_%d" % (e, c)], W=["yz%d" % c], lat=2.0)
            for h, bank in enumerate(("ta", "tb")):
                def tk(g, T, h=h, bank=bank, sm=sm, t=t):
                    for kk in range(8):
                        k = 8 * h + kk
                        o = T[bank][:, CH * kk:CH * kk + CH]
                        g.tensor.matmul(o, T.tp[:, 128 * k:128 * k + 128], sm(T, 6), True, False)
                        r = g.tensor.matmul(o, T.bv[:, 128 * k:128 * k + 128], T[t("vv")][:], False, True)
                    return r
                P(nm("T%d" % h), 16, tk, [t("pp"), t("v"), "tp%d" % (2 * h), "tp%d" % (2 * h + 1)] + ["bv%d" % k for k in range(8 * h, 8 * h + 8)],
                  ["p_" + bank], [bank])
                V(nm("cl%d" % h), 512, lambda g, T, bank=bank, h=h, t=t: g.vector.tensor_scalar(
                    T[t("cc")][:, 512 * h:512 * h + 512], T[bank][:], 0.0, 2048.0, A.max, A.min), ["p_" + bank], [t("cc") + "_%d" % h], [bank])
            for h in range(2):
                def cs(g, T, t=t, h=h):
                    for k in range(8 * h, 8 * h + 8):
                        r = g.tensor.matmul(T.ta[:, 0:CH], h16(T, 0), T[t("cc")][:, CH * k:CH * k + CH], k == 0, k == 15)
                    return r
                P(nm("cs%d" % h), 8, cs, [t("cc") + "_%d" % h, "H0"], ["p_ta"], ["ta"])
            if not last:
                V(nm("kn"), CH, lambda g, T, base=base: g.vector.tensor_scalar(T.kout[:, base:base + CH], T.ta[:, 0:CH], col(T, "kc"), None, A.add),
                  ["p_ta", "c_kc"], ["kout%d_%d" % (e, c)], ["ta"])
                op("G", nm("sk"), 1.0, ("send", "k", e, c, base), R=["kout%d_%d" % (e, c)], W=["sentk%d_%d" % (e + 1, c)])
            else:
                V(nm("kn"), CH, lambda g, T, c=c: g.vector.tensor_scalar(T.ykb[:, CH * c:CH * c + CH], T.ta[:, 0:CH], col(T, "kc"), None, A.add),
                  ["p_ta", "c_kc"], ["ykb%d" % c], ["ta"])
                op("Y", nm("yk"), 0.1, lambda g, T, c=c: g.sync.dma_start(T.yk[:, CH * c:CH * c + CH], T.ykb[:, CH * c:CH * c + CH]),
                   R=["ykb%d" % c], W=["yk%d" % c], lat=2.0)
            P(nm("wb"), 1, lambda g, T, hh=hh: g.tensor.matmul(mr(T, 3), h16(T, 0), hh(T, 3), True, True), [t("b"), "H0", t("sg")], ["m3"], ["bm"])
            V(nm("bfd"), CH, lambda g, T, hh=hh: g.vector.tensor_tensor(hh(T, 2), mr(T, 3), hh(T, 1), A.mult), ["m3", t("fd")], [t("bfd")], ["bm"])

            def pw(g, T, hh=hh):
                g.tensor.matmul(mr(T, 1), h16(T, 0), hh(T, 1), True, False)
                g.tensor.matmul(mr(T, 1), h16(T, 2), hh(T, 2), False, True)
                g.tensor.matmul(mr(T, 2), h16(T, 1), hh(T, 1), True, False)
                return g.tensor.matmul(mr(T, 2), h16(T, 0), hh(T, 2), False, True)
            P(nm("pw"), 4, pw, [t("fd"), t("bfd"), "H0", "H1", "H2"], ["m1", "m2"], ["bm"])
            V(nm("wu"), 2 * CH, lambda g, T, gw=gw: g.vector.tensor_tensor(gw(T, 2, 2), mr(T, 1, 2), gw(T, 2, 2), A.add),
              ["m1", "m2", t("gw2_"), t("gw3_")], [t("gw2_"), t("gw3_")], ["bm"])
            if last:
                o = 2 * CH * c
                V(nm("w0"), CH, lambda g, T, gw=gw, o=o: g.vector.tensor_copy(T.ywb[:, o:o + 2 * CH:2], gw(T, 3)), [t("gw3_")], ["yw0%d" % c])
                V(nm("w1"), 2 * CH, lambda g, T, gw=gw, o=o: g.vector.tensor_tensor(T.ywb[:, o + 1:o + 2 * CH:2], gw(T, 3), gw(T, 2), A.add),
                  [t("gw2_"), t("gw3_")], ["yw1%d" % c])
                op("Y", nm("yw"), 0.1, lambda g, T, o=o: g.sync.dma_start(T.yw[:, o:o + 2 * CH], T.ywb[:, o:o + 2 * CH]),
                   R=["yw0%d" % c, "yw1%d" % c], W=["yw%d" % c], lat=2.0)
            if c == NC - 1 and not last:
                V(nm("fa"), NC, lambda g, T: g.vector.tensor_copy(T.accb[:], T.acc[:]), ["acc%d" % j for j in range(NC)], ["accb"])

                def ft(g, T):
                    for j in range(NC):
                        r = g.tensor.matmul(T.bf[:, 448:449], mat(T, "ONE"), T.accb[:, j:j + 1], j == 0, j == NC - 1)
                    return r
                P(nm("ft"), NC, ft, ["accb", "ONE"], ["f7"], ["bf"])
                V(nm("fi"), 1, lambda g, T: g.vector.tensor_copy(T.fi[:, 0:1], T.bf[:, 448:449]), ["f7"], ["fi"], ["bf"])
                V(nm("fj"), 1, lambda g, T: g.vector.tensor_scalar(T.fj[:, 0:1], T.fi[:, 0:1], 31, None, A.bitwise_and), ["fi"], ["fj"])
                V(nm("tA"), 1, lambda g, T: g.vector.tensor_scalar(col(T, "thA"), T.fj[:, 0:1], 16.0, col(T, "thm"), A.mult, A.add),
                  ["fj", "c_thm"], ["c_thA"])
    return ops


def modulo(ops, per, wgt=None, send=2.5 + 1.1, res=0.01):
    pat = [o for o in ops if o["name"].endswith(".2.0") and o["eng"] in "VSPN"]
    key = {o["k"]: o["name"].split(".")[0] for o in pat}
    succ = {k: [] for k in key}
    for o in pat:
        for d in o["deps"]:
            if d in key:
                succ[d].append(o["k"])
    tail = {}
    for o in reversed(pat):
        k = o["k"]
        tail[k] = o["cost"] + (send if key[k] == "kn" else 0.0) + max([tail[s] + WAKE for s in succ[k]] or [0.0])
    for k in tail:
        tail[k] += (wgt or {}).get(key[k], 0.0)
    npred = {o["k"]: len([d for d in o["deps"] if d in key]) for o in pat}
    ready = [k for k in key if npred[k] == 0]
    use, tau, fin = [], {}, {}
    cells = int(round(per / res))
    eng = {}
    bnk = {}
    while ready:
        k = max(ready, key=lambda x: (tail[x], -x))
        ready.remove(k)
        o = ops[k]
        s = 0.0
        for d in o["deps"]:
            if d in key:
                s = max(s, fin[d] + WAKE)
        if o["eng"] == "N":
            tau[k], fin[k] = 0.0, 0.0 if key[k] == "az" else (wgt or {}).get("AK", 0.6)
        else:
            c0 = int(math.ceil(s / res - 1e-6))
            n = int(math.ceil(o["cost"] / res))
            e = eng.setdefault(o["eng"], set())
            bs = [bnk.setdefault(b, {}) for b in o["banks"]]
            c = c0
            while c < c0 + cells:
                bad = None
                for i in range(c, c + n):
                    m = i % cells
                    if m in e or any(b.get(m, o["eng"]) != o["eng"] for b in bs):
                        bad = i
                        break
                if bad is None:
                    break
                c = bad + 1
            for i in range(c, c + n):
                e.add(i % cells)
                for b in bs:
                    b[i % cells] = o["eng"]
            tau[k], fin[k] = c * res, (c + n) * res
        for x in succ[k]:
            npred[x] -= 1
            if npred[x] == 0:
                ready.append(x)
    return {key[k]: v for k, v in tau.items()}, max(fin[k] for k in key if key[k] == "kn")


def schedule(ops, tau=None, per=0.0):
    n = len(ops)
    succ = [[] for _ in range(n)]
    for o in ops:
        for d in o["deps"] | o["soft"]:
            succ[d].append(o["k"])
    tail = [0.0] * n
    for k in range(n - 1, -1, -1):
        o = ops[k]
        tail[k] = o["cost"] + o["lat"] + max([tail[s] + WAKE for s in succ[k]] or [0.0])
    for k in range(n):
        nme = ops[k]["name"].split(".")
        tail[k] += BIAS.get(nme[0], 0.0)
        if tau and len(nme) == 3:
            tail[k] = -(tau.get(nme[0], 0.0) + per * (NC * int(nme[1]) + int(nme[2])))
    left = [len(o["deps"] | o["soft"]) for o in ops]
    ready = [k for k in range(n) if left[k] == 0]
    end = [None] * n
    free, order = {}, {}
    bank = {}
    while ready:
        cand = {}
        for k in ready:
            o = ops[k]
            s = free.get(o["eng"], 0.0) if o["eng"] != "N" else 0.0
            for d in o["deps"] | o["soft"]:
                w = 0.0 if (ops[d]["eng"] == o["eng"] and d not in o["deps"]) else WAKE
                s = max(s, end[d] + ops[d]["lat"] + w)
            for b in o["banks"]:
                for q, x in bank.get(b, {}).items():
                    if q != o["eng"]:
                        s = max(s, end[x] + WAKE)
            cand.setdefault(o["eng"], []).append((s, k))
        best = None
        for q, l in cand.items():
            s0 = min(l)[0]
            s, k = max((x for x in l if x[0] <= s0 + AHEAD), key=lambda x: (tail[x[1]], -x[1]))
            if best is None or s0 < best[0]:
                best = (s0, s, k)
        _, s, k = best
        o = ops[k]
        end[k] = s + o["cost"]
        if o["eng"] != "N":
            free[o["eng"]] = end[k]
        order.setdefault(o["eng"], []).append(k)
        o["start"] = s
        for b in o["banks"]:
            u = bank.setdefault(b, {})
            for q, x in u.items():
                if q != o["eng"]:
                    o["soft"].add(x)
            u[o["eng"]] = k
        ready.remove(k)
        for x in succ[k]:
            left[x] -= 1
            if left[x] == 0:
                ready.append(x)
    return order, end


for _c in range(NC):
    SCRATCH["vv%d" % _c] = ("sbuf", [128, CH], "float16")
PLAN = {}


def plan():
    if "ops" not in PLAN:
        ops = build()
        order, end = schedule(ops)
        glob = sorted((o["start"], o["k"]) for o in ops)
        PLAN["ops"] = ops
        PLAN["glob"] = [k for _, k in glob]
        PLAN["end"] = end
        cnt = {}
        for q, l in order.items():
            c = 0
            for k in l:
                o = ops[k]
                if q in SEM and not (q == "G" and isinstance(o["fn"], tuple)):
                    c += 1
                o["cnt"] = c
            cnt[q] = c
        PLAN["order"], PLAN["cnt"] = order, cnt
    return PLAN


def rank_program(g, core, T, topo):
    rank = T.rank_of(core)
    if rank is None:
        return
    pl = plan()
    ops, order = pl["ops"], pl["order"]
    nxt = T.cores[(rank + 1) % len(T.cores)]
    prv = T.cores[(rank - 1) % len(T.cores)]
    rid, pid = topo.addr(nxt, core)
    mask = topo.mask(core, nxt)
    neng = len(topo.engines(core, nxt))
    narr = len(topo.engines(prv, core))
    que = {"V": g.vector, "S": g.scalar, "P": g.tensor, "G": g, "Y": g.sync}

    for x, q, dst in (("gx", g.scalar, T.gxb[:]), ("rk", g.sync, T.rkb[:]), ("z0", g.sync, T.zin[:, 0:192]), ("wt", g.sync, T.wtb[:]),
                      ("rt", g.sync, T.rtb[:]), ("sy", g.scalar, T.syb[:]), ("wr", g.sync, T.wrb[:]), ("th", g.sync, T.thb[:])):
        q.dma_start(dst, T[x][:]).then_inc(T.sem["ld_" + x], 16)

    know = {q: {} for q in que}
    snap = {}
    fin = [0]

    def need(q, k, hard):
        o = ops[k]
        if o["eng"] == "N":
            nme, v = o["sem"]
            return nme, v if v else narr
        if o["eng"] == q and not hard:
            return None
        return SEM[o["eng"]], o["cnt"]

    for k in pl["glob"]:
        o = ops[k]
        q = o["eng"]
        if q == "N":
            s = {}
            for d in o["deps"]:
                pass
            snap[k] = s
            continue
        req = {}
        for d, hard in [(d, True) for d in o["deps"]] + [(d, False) for d in o["soft"]]:
            if ops[d]["eng"] == "G" and isinstance(ops[d]["fn"], tuple):
                continue
            r = need(q, d, hard)
            if r is None:
                continue
            req.setdefault(r[0], (0, None))
            if r[1] > req[r[0]][0]:
                req[r[0]] = (r[1], d)
        kn = know[q]
        for nme, (v, d) in sorted(req.items(), key=lambda x: -ops[x[1][1]].get("start", 0.0)):
            if kn.get(nme, 0) >= v:
                continue
            que[q].wait_ge(T.sem[nme], v)
            for a, b in snap[d].items():
                if kn.get(a, 0) < b:
                    kn[a] = b
            kn[nme] = max(kn.get(nme, 0), v)
        if isinstance(o["fn"], tuple):
            _, kind, e, c, base = o["fn"]
            src, dst = (T.zout, T.zin) if kind == "z" else (T.kout, T.kin)
            b2 = 192 * (e + 1) + CH * c
            g.remote_dma(dst[:, b2:b2 + CH], src[:, base:base + CH], T.sem["a%s%d_%d" % (kind, e + 1, c)], T.sem.loc, pid, rid, mask)
            fin[0] += neng
        else:
            ins = o["fn"](g, T)
            if q == "Y":
                ins.then_inc(T.sem.fin, 16)
            else:
                ins.then_inc(T.sem[SEM[q]], 1)
        snap[k] = dict(kn)
    g.wait_ge(T.sem.loc, fin[0])
    g.wait_ge(T.sem.fin, 16 * len(order["Y"]))
    for q, s in SEM.items():
        g.wait_ge(T.sem[s], pl["cnt"][q])
    for o in ops:
        if o["eng"] == "N":
            nme, v = o["sem"]
            g.wait_ge(T.sem[nme], v if v else narr)
